import numpy as np
import ml_dtypes


def mxq(x, axis, fmt="e4m3"):
    dtype, down = {"e4m3": (ml_dtypes.float8_e4m3fn, 7), "e5m2": (ml_dtypes.float8_e5m2, 14)}[fmt]
    v = np.moveaxis(np.asarray(x, np.float32).astype(ml_dtypes.bfloat16).astype(np.float64), axis, -1)
    blocks = v.reshape(v.shape[:-1] + (-1, 32))
    amax = np.abs(blocks).max(-1, keepdims=True)
    byte = np.maximum(np.where(amax > 0, np.frexp(amax)[1] - 1 + 127, 0) - down, 1)
    scale = np.exp2(byte - 127.0)
    codes = (blocks / scale).astype(np.float32).astype(dtype).astype(np.float64)
    return np.moveaxis((codes * scale).reshape(v.shape), -1, axis)


WIDE = False


def mx_kscale(k):
    if not WIDE:
        return np.ones(k)
    levels = np.array([10, -10, 5, -5, 0])
    if k % 512:
        return np.exp2(np.random.permutation(np.resize(levels, k // 32))).repeat(32)
    a = np.empty((k // 512, 16))
    for p in range(k // 512):
        a[p, :8] = np.random.permutation(np.resize(levels, 8))
        for g in range(8):
            far = levels[np.abs(levels - a[p, g]) >= 10]
            a[p, g + 8] = far[np.random.randint(len(far))]
    return np.exp2(a.ravel()).repeat(32)


def f64(x):
    return np.asarray(x).astype(np.float64)


def striped(idx):
    return np.tile(np.asarray(idx).reshape(-1, 16).T, (8, 1)).astype(np.uint16)


def unstriped(offs):
    return offs[:16].T.reshape(-1).astype(np.int64)


E2M1 = np.array([0.0, 0.5, 1.0, 1.5, 2.0, 3.0, 4.0, 6.0, -0.0, -0.5, -1.0, -1.5, -2.0, -3.0, -4.0, -6.0])


def pack_weight(w, fmt):
    k, n = w.shape
    w = f64(np.asarray(w, np.float32).astype(ml_dtypes.bfloat16)).reshape(k // 32, 32, n)
    amax = np.abs(w).max(1)
    if fmt == "e4m3":
        byte = np.frexp(amax)[1] - 1 + 127 - 7
    else:
        mant, ex = np.frexp(amax / 6.0)
        byte = np.where(mant > 0.5, ex, ex - 1) + 127
    byte = np.clip(np.where(amax > 0, byte, 1), 1, 254)
    scaled = (w * np.exp2(127.0 - byte)[:, None, :]).reshape(k, n).astype(np.float32)
    by_word = np.ascontiguousarray(scaled.reshape(k // 512, 128, 4, n).transpose(0, 1, 3, 2))
    if fmt == "e4m3":
        words = by_word.astype(ml_dtypes.float8_e4m3fn).view(np.uint8)
    else:
        c = by_word.astype(ml_dtypes.float4_e2m1fn).view(np.uint8) & 0xF
        words = (c[..., 0::2] | (c[..., 1::2] << 4)).reshape(k // 512, 128, 2 * n)
    return np.ascontiguousarray(words), np.ascontiguousarray(byte.astype(np.uint8).reshape(k // 512, 16, n))


def unpack_weight(words, scales, fmt):
    g, _, n = scales.shape
    words = np.ascontiguousarray(words).reshape(g, 128, n, -1)
    if fmt == "e4m3":
        vals = words.view(ml_dtypes.float8_e4m3fn).astype(np.float64)
    else:
        nib = np.empty((g, 128, n, 4), np.uint8)
        nib[..., 0::2] = words & 0xF
        nib[..., 1::2] = words >> 4
        vals = E2M1[nib]
    vals = vals * np.repeat(np.exp2(scales.astype(np.float64) - 127.0), 8, axis=1)[..., None]
    return vals.transpose(0, 1, 3, 2).reshape(g * 512, n)


def silu(v):
    return v / (1.0 + np.exp(-v))


def bf(x):
    return np.asarray(x, np.float32).astype(ml_dtypes.bfloat16)


def planes(Y):
    r, m = Y.shape
    b = f64(bf(Y)).reshape(r // 32, 32, m)
    amax = np.abs(b).max(1)
    byte = np.clip(np.where(amax > 0, np.frexp(amax)[1] - 1 + 127 - 7, 1), 1, 254)
    codes = (b * np.exp2(127.0 - byte)[:, None, :]).reshape(r, m).astype(np.float32).astype(ml_dtypes.float8_e4m3fn).view(np.uint8)
    words = codes.reshape(r // 512, 128, 4, m).transpose(0, 1, 3, 2)
    return np.ascontiguousarray(words), np.ascontiguousarray(byte.astype(np.uint8).reshape(r // 512, 16, m))


B, N, T, D, NQ = 1, 512, 2048, 1024, 512


def setup_inputs():
    n = np.random.standard_normal
    idx = np.random.permutation(T)[:B * N]
    s = mx_kscale(D)[:, None]
    kp = pack_weight(n((D, T)) / s, "e2m1")
    cp = pack_weight(n((D, T)) / s, "e2m1")
    return {
        "qT": (n((B, D, NQ)) * s * (1.00 / np.sqrt(D))).astype(np.float32),
        "k_words": np.ascontiguousarray(kp[0].reshape(1, 2, 128, T, 2).transpose(0, 2, 3, 1, 4)).reshape(1, 128, T, 4),
        "k_scales": kp[1],
        "c_words": np.ascontiguousarray(cp[0].reshape(1, 2, 128, T, 2).transpose(0, 2, 3, 1, 4)).reshape(1, 128, T, 4),
        "c_scales": cp[1],
        "nb": np.tile(0.5 * n(2048), (128, 1)).astype(np.float32),
        "offs": striped(idx),
    }


def reference(qT, k_words, k_scales, c_words, c_scales, nb, offs):
    idx = unstriped(offs)
    pick = lambda x, which: x[:, which].reshape(x.shape[0], B, -1).transpose(1, 0, 2)
    k = unpack_weight(k_words.reshape(1, 128, T, 2, 2).transpose(0, 3, 1, 2, 4).reshape(2, 128, 2 * T), k_scales, "e2m1")
    kg = pick(k, idx)
    c = unpack_weight(c_words.reshape(1, 128, T, 2, 2).transpose(0, 3, 1, 2, 4).reshape(2, 128, 2 * T), c_scales, "e2m1")
    cg = pick(c, idx)
    qq = mxq(f64(qT), 1, "e4m3")
    a = kg.transpose(0, 2, 1) @ qq
    z = cg.transpose(0, 2, 1) @ qq
    y = silu(a + pick(f64(nb), idx)[:, :1, :].transpose(0, 2, 1)) * z
    Y = y[0]
    words, scales = planes(Y)
    return Y, words, scales

@@ -1,0 +1,155 @@
+from contextlib import ExitStack
+
+import concourse.mybir as mybir
+from concourse.masks import make_identity
+
+N, T, D, NQ = 512, 2048, 1024, 512
+FLOPS = 2 * 2 * N * NQ * D
+
+F32 = mybir.dt.float32
+BF16 = mybir.dt.bfloat16
+I32 = mybir.dt.int32
+U32 = mybir.dt.uint32
+U16 = mybir.dt.uint16
+U8 = mybir.dt.uint8
+FP8X4 = mybir.dt.float8_e4m3fn_x4
+FP4X4 = mybir.dt.float4_e2m1fn_x4
+SILU = mybir.ActivationFunctionType.Silu
+MULT = mybir.AluOpType.mult
+
+P = 128
+PACK = 4
+PASSES = 2
+HALF = NQ // 2
+BIAS_ROW = P - 1
+SCALE_ROW = 96
+
+
+def interleave_views(dst, src):
+    return (dst.rearrange("p (c i) t -> p c t i", i=4), src.rearrange("p t (c i) -> p c t i", i=4))
+
+
+def tile_attend_plh_bswiglu_topk_kernel(tc, qT, k_words, k_scales, c_words, c_scales, nb, offs, out_0, out_1, out_2):
+    nc = tc.nc
+    with ExitStack() as ctx:
+        sb = ctx.enter_context(tc.tile_pool(name="sb", bufs=1))
+        psum = ctx.enter_context(tc.psum_pool(name="psum", bufs=1))
+
+        offsets = sb.tile([P, N // 16], U16, name="offsets")
+        nb_pool = sb.tile([P, T], F32, name="nb_pool")
+        kw_pool = sb.tile([P, T], I32, name="kw_pool")
+        cw_pool = sb.tile([P, T], I32, name="cw_pool")
+        ks_pool = sb.tile([P, T], U8, name="ks_pool")
+        cs_pool = sb.tile([P, T], U8, name="cs_pool")
+        q_raw = [sb.tile([P, PACK, NQ], F32, name="q_raw%d" % o) for o in range(PASSES)]
+
+        nc.vector.memset(ks_pool[0:SCALE_ROW, :].bitcast(I32), 0)
+        nc.vector.memset(cs_pool[0:SCALE_ROW, :].bitcast(I32), 0)
+        nc.vector.memset(nb_pool[0:BIAS_ROW, :], 0.0)
+
+        nc.sync.dma_start(offsets[:], offs)
+        nc.sync.dma_start(ks_pool[SCALE_ROW:P, :].bitcast(I32), k_scales.rearrange("o f t -> f o t").bitcast(I32))
+        nc.sync.dma_start(cs_pool[SCALE_ROW:P, :].bitcast(I32), c_scales.rearrange("o f t -> f o t").bitcast(I32))
+        nc.sync.dma_start(nb_pool[BIAS_ROW:P, :], nb[0:1, :])
+        for o, (pool, words) in enumerate(((kw_pool, k_words), (cw_pool, c_words))):
+            nc.sync.dma_start(q_raw[o][:], qT[0, 512 * o : 512 * (o + 1), :].rearrange("(p j) w -> p j w", j=PACK))
+            nc.sync.dma_start(pool[:], words[0].rearrange("p t b -> p (t b)").bitcast(I32))
+
+        ident = sb.tile([P, P], F32, name="ident")
+        make_identity(nc, ident[:])
+
+        def listed_scales(name, pool, queues):
+            planes = sb.tile([P, PASSES, N], U8, name=name + "_planes", align_bytes=64)
+            nc.gpsimd.memset(planes[:].bitcast(I32), 0)
+            picked = sb.tile([P, N], U8, name=name + "_picked")
+            nc.vector.tensor_copy(picked[:], pool[:].indirect(offsets[:]))
+            dealt = sb.tile([P, N], U8, name=name + "_dealt")
+            nc.vector.tensor_copy(dealt[:].rearrange("p (r s) -> p s r", r=PACK), picked[:].rearrange("p (s r) -> p s r", r=PACK))
+            for quad in range(4):
+                first = SCALE_ROW + 8 * quad
+                queues[quad].dma_start(planes[32 * quad : 32 * quad + 4, :, :].bitcast(I32), dealt[first : first + 8, :].bitcast(I32))
+            return planes
+
+        k_planes = listed_scales("ks", ks_pool, [nc.gpsimd, nc.scalar, nc.scalar, nc.scalar])
+        c_planes = listed_scales("cs", cs_pool, [nc.sync] * 4)
+
+        nb_picked = sb.tile([P, N], F32, name="nb_picked")
+        nc.vector.tensor_copy(nb_picked[:], nb_pool[:].indirect(offsets[:]))
+        nb_turned = psum.tile([P, PACK, P], F32, name="nb_turned", tag="z3")
+        for r in range(PACK):
+            nc.tensor.transpose(nb_turned[:, r, :], nb_picked[:, r:N:PACK], ident[:])
+        bias = sb.tile([P, PACK], F32, name="bias")
+        nc.scalar.copy(bias[:], nb_turned[:, :, BIAS_ROW])
+
+        kw_picked = sb.tile([P, N], U32, name="kw_picked")
+        nc.vector.tensor_copy(kw_picked[:], kw_pool[:].bitcast(U32).indirect(offsets[:]))
+        kw_halves = kw_picked[:].bitcast(U16).rearrange("p (s r o) -> p o s r", r=PACK, o=PASSES)
+        k_codes = [sb.tile([P, 2 * N], U8, name="k_codes%d" % o, align_bytes=64) for o in range(PASSES)]
+        for o in range(PASSES):
+            nc.vector.tensor_copy(k_codes[o][:].bitcast(U16).rearrange("p (r s) -> p s r", r=PACK), kw_halves[:, o, :, :])
+
+        q_codes = [sb.tile([P, NQ], U32, name="q_codes%d" % o, align_bytes=64) for o in range(PASSES)]
+        q_planes = [sb.tile([P, NQ], U8, name="q_plane%d" % o, align_bytes=64) for o in range(PASSES)]
+        q0_bf = sb.tile([P, NQ, PACK], BF16, name="q0_bf", align_bytes=64)
+        nc.scalar.copy(*interleave_views(q0_bf[:], q_raw[0][:]))
+        nc.vector.quantize_mx(out=q_codes[0][:].bitcast(FP8X4), scales=q_planes[0][:], in_=q0_bf[:].rearrange("p w j -> p (w j)"))
+        q1_bf = [sb.tile([P, HALF, PACK], BF16, name="q1_bf%d" % h, align_bytes=64) for h in range(2)]
+        nc.vector.tensor_copy(*interleave_views(q1_bf[0][:], q_raw[1][:, :, 0:HALF]))
+        nc.scalar.copy(*interleave_views(q1_bf[1][:], q_raw[1][:, :, HALF:NQ]))
+        for h in range(2):
+            cols = slice(h * HALF, (h + 1) * HALF)
+            nc.vector.quantize_mx(out=q_codes[1][:, cols].bitcast(FP8X4), scales=q_planes[1][:, cols], in_=q1_bf[h][:].rearrange("p w j -> p (w j)"))
+
+        gate_banks = [psum.tile([P, NQ], F32, name="gate%d" % r, tag="a%d" % r) for r in range(PACK)]
+        for o in range(PASSES):
+            for r in range(PACK):
+                nc.tensor.matmul_mx(
+                    out=gate_banks[r][:],
+                    lhsT=k_codes[o][:, 2 * P * r : 2 * P * (r + 1)].bitcast(FP4X4),
+                    lhsT_scale=k_planes[:, o, P * r : P * (r + 1)],
+                    rhs=q_codes[o][:].bitcast(FP8X4),
+                    rhs_scale=q_planes[o][:],
+                    start=(o == 0),
+                    stop=(o == PASSES - 1),
+                )
+        gates = [sb.tile([P, NQ], F32, name="gates%d" % r) for r in range(PACK)]
+        for r in range(PACK):
+            nc.scalar.activation(gates[r][:], gate_banks[r][:], SILU, bias=bias[:, r : r + 1])
+
+        cw_picked = sb.tile([P, N], U32, name="cw_picked")
+        nc.vector.tensor_copy(cw_picked[:], cw_pool[:].bitcast(U32).indirect(offsets[:]))
+        cw_halves = cw_picked[:].bitcast(U16).rearrange("p (s r o) -> p r s o", r=PACK, o=PASSES)
+        c_codes = [sb.tile([P, PASSES, 2 * P], U8, name="c_codes%d" % r, align_bytes=64) for r in range(PACK)]
+        for r in range(PACK):
+            nc.vector.tensor_copy(c_codes[r][:].bitcast(U16).rearrange("p o s -> p s o"), cw_halves[:, r, :, :])
+
+        y = sb.tile([P, PACK, NQ], F32, name="y")
+        out_rows = out_0.rearrange("(p r) q -> p r q", r=PACK)
+        for r in range(PACK):
+            lin_bank = psum.tile([P, NQ], F32, name="lin%d" % r, tag="z%d" % r)
+            for o in range(PASSES):
+                nc.tensor.matmul_mx(
+                    out=lin_bank[:],
+                    lhsT=c_codes[r][:, o, :].bitcast(FP4X4),
+                    lhsT_scale=c_planes[:, o, P * r : P * (r + 1)],
+                    rhs=q_codes[o][:].bitcast(FP8X4),
+                    rhs_scale=q_planes[o][:],
+                    start=(o == 0),
+                    stop=(o == PASSES - 1),
+                )
+            nc.vector.tensor_tensor(y[:, r, :], lin_bank[:], gates[r][:], MULT)
+            nc.sync.dma_start(out_rows[:, r, :], y[:, r, :])
+
+        y_codes = sb.tile([P, NQ], U32, name="y_codes", align_bytes=64)
+        y_plane = sb.tile([P, NQ], U8, name="y_plane", align_bytes=64)
+        y_bf = [sb.tile([P, HALF, PACK], BF16, name="y_bf%d" % h, align_bytes=64) for h in range(2)]
+        nc.vector.tensor_copy(*interleave_views(y_bf[0][:], y[:, :, 0:HALF]))
+        nc.scalar.copy(*interleave_views(y_bf[1][:], y[:, :, HALF:NQ]))
+        words_out = out_1[0].rearrange("p q b -> p (q b)").bitcast(I32)
+        for h in range(2):
+            cols = slice(h * HALF, (h + 1) * HALF)
+            nc.vector.quantize_mx(out=y_codes[:, cols].bitcast(FP8X4), scales=y_plane[:, cols], in_=y_bf[h][:].rearrange("p w j -> p (w j)"))
+            nc.sync.dma_start(words_out[:, cols], y_codes[:, cols].bitcast(I32))
+        for quad in range(4):
+            queue = nc.scalar if quad % 2 else nc.sync
+            queue.dma_start(out_2[0, 4 * quad : 4 * quad + 4, :].bitcast(I32), y_plane[32 * quad : 32 * quad + 4, :].bitcast(I32))

@@ -23,6 +23,8 @@ PASSES = 2
 HALF = NQ // 2
 BIAS_ROW = P - 1
 SCALE_ROW = 96
+SHARE = 96
+WARM_PASSES = 3
 
 
 def interleave_views(dst, src):
@@ -37,11 +39,16 @@ def tile_attend_plh_bswiglu_topk_kernel(tc, qT, k_words, k_scales, c_words, c_sc
 
         offsets = sb.tile([P, N // 16], U16, name="offsets")
         nb_pool = sb.tile([P, T], F32, name="nb_pool")
-        kw_pool = sb.tile([P, T], I32, name="kw_pool")
+        kw_pool = sb.tile([P, T], I32, name="kw_pool", align_bytes=64)
         cw_pool = sb.tile([P, T], I32, name="cw_pool")
-        ks_pool = sb.tile([P, T], U8, name="ks_pool")
-        cs_pool = sb.tile([P, T], U8, name="cs_pool")
-        q_raw = [sb.tile([P, PACK, NQ], F32, name="q_raw%d" % o) for o in range(PASSES)]
+        ks_pool = sb.tile([P, T], U8, name="ks_pool", align_bytes=64)
+        cs_pool = sb.tile([P, T], U8, name="cs_pool", tag="late0", align_bytes=64)
+        q0_raw = sb.tile([P, PACK, NQ], F32, name="q0_raw")
+
+        warm_in = sb.tile([P, 1], F32, name="warm_in")
+        warm_out = sb.tile([P, 1], F32, name="warm_out")
+        nc.gpsimd.memset(warm_in[:], 0.0)
+        nc.scalar.activation(warm_out[:], warm_in[:], SILU)
 
         nc.vector.memset(ks_pool[0:SCALE_ROW, :].bitcast(I32), 0)
         nc.vector.memset(cs_pool[0:SCALE_ROW, :].bitcast(I32), 0)
@@ -51,102 +58,136 @@ def tile_attend_plh_bswiglu_topk_kernel(tc, qT, k_words, k_scales, c_words, c_sc
         nc.sync.dma_start(ks_pool[SCALE_ROW:P, :].bitcast(I32), k_scales.rearrange("o f t -> f o t").bitcast(I32))
         nc.sync.dma_start(cs_pool[SCALE_ROW:P, :].bitcast(I32), c_scales.rearrange("o f t -> f o t").bitcast(I32))
         nc.sync.dma_start(nb_pool[BIAS_ROW:P, :], nb[0:1, :])
-        for o, (pool, words) in enumerate(((kw_pool, k_words), (cw_pool, c_words))):
-            nc.sync.dma_start(q_raw[o][:], qT[0, 512 * o : 512 * (o + 1), :].rearrange("(p j) w -> p j w", j=PACK))
+        q_rows = qT[0].rearrange("(o p j) w -> o p j w", o=PASSES, j=PACK)
+        nc.sync.dma_start(q0_raw[:], q_rows[0])
+        for pool, words in ((kw_pool, k_words), (cw_pool, c_words)):
             nc.sync.dma_start(pool[:], words[0].rearrange("p t b -> p (t b)").bitcast(I32))
 
         ident = sb.tile([P, P], F32, name="ident")
         make_identity(nc, ident[:])
 
-        def listed_scales(name, pool, queues):
+        def gather_scales(name, pool, tag):
+            picked = sb.tile([P, N], U8, name=name + "_picked", tag=tag, align_bytes=64)
+            nc.vector.tensor_copy(picked[:], pool[:].indirect(offsets[:]))
+            return picked
+
+        def place_scales(name, picked):
             planes = sb.tile([P, PASSES, N], U8, name=name + "_planes", align_bytes=64)
             nc.gpsimd.memset(planes[:].bitcast(I32), 0)
-            picked = sb.tile([P, N], U8, name=name + "_picked")
-            nc.vector.tensor_copy(picked[:], pool[:].indirect(offsets[:]))
             dealt = sb.tile([P, N], U8, name=name + "_dealt")
-            nc.vector.tensor_copy(dealt[:].rearrange("p (r s) -> p s r", r=PACK), picked[:].rearrange("p (s r) -> p s r", r=PACK))
+            nc.vector.tensor_copy(dealt[:].rearrange("p (r s) -> p r s", r=PACK), picked[:].rearrange("p (s r) -> p r s", r=PACK))
             for quad in range(4):
                 first = SCALE_ROW + 8 * quad
-                queues[quad].dma_start(planes[32 * quad : 32 * quad + 4, :, :].bitcast(I32), dealt[first : first + 8, :].bitcast(I32))
+                nc.scalar.dma_start(planes[32 * quad : 32 * quad + 4, :, :].bitcast(I32), dealt[first : first + 8, :].bitcast(I32))
             return planes
 
-        k_planes = listed_scales("ks", ks_pool, [nc.gpsimd, nc.scalar, nc.scalar, nc.scalar])
-        c_planes = listed_scales("cs", cs_pool, [nc.sync] * 4)
-
+        ks_picked = gather_scales("ks", ks_pool, "ks_picked")
+        cs_picked = gather_scales("cs", cs_pool, "late1")
+        k_planes = place_scales("ks", ks_picked)
         nb_picked = sb.tile([P, N], F32, name="nb_picked")
         nc.vector.tensor_copy(nb_picked[:], nb_pool[:].indirect(offsets[:]))
+        c_planes = place_scales("cs", cs_picked)
+
+        q1_raw = [sb.tile([P, PACK, HALF], F32, name="q1_raw%d" % h, tag="late%d" % h, align_bytes=64) for h in range(2)]
+        for h in range(2):
+            nc.sync.dma_start(q1_raw[h][:], q_rows[1][:, :, h * HALF : (h + 1) * HALF])
+
         nb_turned = psum.tile([P, PACK, P], F32, name="nb_turned", tag="z3")
         for r in range(PACK):
             nc.tensor.transpose(nb_turned[:, r, :], nb_picked[:, r:N:PACK], ident[:])
         bias = sb.tile([P, PACK], F32, name="bias")
         nc.scalar.copy(bias[:], nb_turned[:, :, BIAS_ROW])
 
-        kw_picked = sb.tile([P, N], U32, name="kw_picked")
-        nc.vector.tensor_copy(kw_picked[:], kw_pool[:].bitcast(U32).indirect(offsets[:]))
-        kw_halves = kw_picked[:].bitcast(U16).rearrange("p (s r o) -> p o s r", r=PACK, o=PASSES)
-        k_codes = [sb.tile([P, 2 * N], U8, name="k_codes%d" % o, align_bytes=64) for o in range(PASSES)]
-        for o in range(PASSES):
-            nc.vector.tensor_copy(k_codes[o][:].bitcast(U16).rearrange("p (r s) -> p s r", r=PACK), kw_halves[:, o, :, :])
+        def gather_words(name, pool):
+            picked = sb.tile([P, N], U32, name=name + "_picked")
+            nc.vector.tensor_copy(picked[:], pool[:].bitcast(U32).indirect(offsets[:]))
+            return picked[:].bitcast(U16).rearrange("p (s r o) -> p o s r", r=PACK, o=PASSES)
+
+        def deal_words(name, halves, o, first, count, tag=""):
+            codes = sb.tile([P, count, 2 * P], U8, name="%s_codes%d_%d" % (name, o, first), tag=tag, align_bytes=64)
+            nc.vector.tensor_copy(codes[:].bitcast(U16).rearrange("p r s -> p s r"), halves[:, o, :, first : first + count])
+            return [codes[:, i, :] for i in range(count)]
 
         q_codes = [sb.tile([P, NQ], U32, name="q_codes%d" % o, align_bytes=64) for o in range(PASSES)]
         q_planes = [sb.tile([P, NQ], U8, name="q_plane%d" % o, align_bytes=64) for o in range(PASSES)]
+
         q0_bf = sb.tile([P, NQ, PACK], BF16, name="q0_bf", align_bytes=64)
-        nc.scalar.copy(*interleave_views(q0_bf[:], q_raw[0][:]))
+        nc.scalar.copy(*interleave_views(q0_bf[:], q0_raw[:]))
         nc.vector.quantize_mx(out=q_codes[0][:].bitcast(FP8X4), scales=q_planes[0][:], in_=q0_bf[:].rearrange("p w j -> p (w j)"))
-        q1_bf = [sb.tile([P, HALF, PACK], BF16, name="q1_bf%d" % h, align_bytes=64) for h in range(2)]
-        nc.vector.tensor_copy(*interleave_views(q1_bf[0][:], q_raw[1][:, :, 0:HALF]))
-        nc.scalar.copy(*interleave_views(q1_bf[1][:], q_raw[1][:, :, HALF:NQ]))
+        warm_bank = psum.tile([P, NQ], F32, name="warm_bank", tag="z2")
+        for i in range(WARM_PASSES):
+            nc.tensor.matmul_mx(
+                out=warm_bank[:],
+                lhsT=kw_pool[:, 0 : P // 2].bitcast(FP4X4),
+                lhsT_scale=ks_pool[:, 0:P],
+                rhs=q_codes[0][:].bitcast(FP8X4),
+                rhs_scale=q_planes[0][:],
+                start=True,
+                stop=True,
+            )
+        k_halves = gather_words("kw", kw_pool)
+        k_codes = [deal_words("kw", k_halves, 0, 0, PACK)]
+        c_halves = gather_words("cw", cw_pool)
+        c_codes = [deal_words("cw", c_halves, 0, 0, 2)]
+        k_codes.append(deal_words("kw", k_halves, 1, 0, 2))
+
+        q1_bf = [sb.tile([P, HALF, PACK], BF16, name="q1_bf%d" % h, tag="q1_bf%d" % h, align_bytes=64) for h in range(2)]
+        nc.scalar.copy(*interleave_views(q1_bf[0][:], q1_raw[0][:]))
+        nc.scalar.copy(*interleave_views(q1_bf[1][:, 0:SHARE, :], q1_raw[1][:, :, 0:SHARE]))
+        nc.vector.tensor_copy(*interleave_views(q1_bf[1][:, SHARE:HALF, :], q1_raw[1][:, :, SHARE:HALF]))
         for h in range(2):
             cols = slice(h * HALF, (h + 1) * HALF)
             nc.vector.quantize_mx(out=q_codes[1][:, cols].bitcast(FP8X4), scales=q_planes[1][:, cols], in_=q1_bf[h][:].rearrange("p w j -> p (w j)"))
+        c_codes.append(deal_words("cw", c_halves, 1, 0, 2, "late1"))
+        k_codes[1].extend(deal_words("kw", k_halves, 1, 2, 2, "q1_bf0"))
+        c_late = sb.tile([P, PASSES, 2, 2 * P], U8, name="cw_codes_late", tag="q1_bf1", align_bytes=64)
+        nc.vector.tensor_copy(c_late[:].bitcast(U16).rearrange("p o r s -> p s r o"), c_halves[:, :, :, 2:PACK].rearrange("p o s r -> p s r o"))
+        for o in range(PASSES):
+            c_codes[o].extend([c_late[:, o, i, :] for i in range(2)])
 
         gate_banks = [psum.tile([P, NQ], F32, name="gate%d" % r, tag="a%d" % r) for r in range(PACK)]
-        for o in range(PASSES):
-            for r in range(PACK):
-                nc.tensor.matmul_mx(
-                    out=gate_banks[r][:],
-                    lhsT=k_codes[o][:, 2 * P * r : 2 * P * (r + 1)].bitcast(FP4X4),
-                    lhsT_scale=k_planes[:, o, P * r : P * (r + 1)],
-                    rhs=q_codes[o][:].bitcast(FP8X4),
-                    rhs_scale=q_planes[o][:],
-                    start=(o == 0),
-                    stop=(o == PASSES - 1),
-                )
-        gates = [sb.tile([P, NQ], F32, name="gates%d" % r) for r in range(PACK)]
-        for r in range(PACK):
-            nc.scalar.activation(gates[r][:], gate_banks[r][:], SILU, bias=bias[:, r : r + 1])
+        lin_banks = [psum.tile([P, NQ], F32, name="lin%d" % r, tag="z%d" % r) for r in range(PACK)]
 
-        cw_picked = sb.tile([P, N], U32, name="cw_picked")
-        nc.vector.tensor_copy(cw_picked[:], cw_pool[:].bitcast(U32).indirect(offsets[:]))
-        cw_halves = cw_picked[:].bitcast(U16).rearrange("p (s r o) -> p r s o", r=PACK, o=PASSES)
-        c_codes = [sb.tile([P, PASSES, 2 * P], U8, name="c_codes%d" % r, align_bytes=64) for r in range(PACK)]
-        for r in range(PACK):
-            nc.vector.tensor_copy(c_codes[r][:].bitcast(U16).rearrange("p o s -> p s o"), cw_halves[:, r, :, :])
+        def mx_pass(bank, codes, planes, o, r):
+            nc.tensor.matmul_mx(
+                out=bank[:],
+                lhsT=codes[o][r].bitcast(FP4X4),
+                lhsT_scale=planes[:, o, P * r : P * (r + 1)],
+                rhs=q_codes[o][:].bitcast(FP8X4),
+                rhs_scale=q_planes[o][:],
+                start=(o == 0),
+                stop=(o == PASSES - 1),
+            )
 
-        y = sb.tile([P, PACK, NQ], F32, name="y")
-        out_rows = out_0.rearrange("(p r) q -> p r q", r=PACK)
         for r in range(PACK):
-            lin_bank = psum.tile([P, NQ], F32, name="lin%d" % r, tag="z%d" % r)
-            for o in range(PASSES):
-                nc.tensor.matmul_mx(
-                    out=lin_bank[:],
-                    lhsT=c_codes[r][:, o, :].bitcast(FP4X4),
-                    lhsT_scale=c_planes[:, o, P * r : P * (r + 1)],
-                    rhs=q_codes[o][:].bitcast(FP8X4),
-                    rhs_scale=q_planes[o][:],
-                    start=(o == 0),
-                    stop=(o == PASSES - 1),
-                )
-            nc.vector.tensor_tensor(y[:, r, :], lin_bank[:], gates[r][:], MULT)
-            nc.sync.dma_start(out_rows[:, r, :], y[:, r, :])
+            mx_pass(gate_banks[r], k_codes, k_planes, 0, r)
+        for r in range(2):
+            mx_pass(lin_banks[r], c_codes, c_planes, 0, r)
+
+        y = sb.tile([P, 2, PACK, HALF], F32, name="y")
+        out_rows = out_0.rearrange("(p r) (h q) -> p r h q", r=PACK, h=2)
+        mx_pass(gate_banks[0], k_codes, k_planes, 1, 0)
+        for r in range(PACK):
+            if r + 1 < PACK:
+                mx_pass(gate_banks[r + 1], k_codes, k_planes, 1, r + 1)
+            for o in range(1 if r < 2 else 0, PASSES):
+                mx_pass(lin_banks[r], c_codes, c_planes, o, r)
+            gates = sb.tile([P, NQ], F32, name="gates%d" % r)
+            lin = lin_banks[r][:].rearrange("p (h q) -> p h q", h=2)
+            gate = gates[:].rearrange("p (h q) -> p h q", h=2)
+            pre = gate_banks[r][:].rearrange("p (h q) -> p h q", h=2)
+            for hs in ([slice(0, 2)] if r < PACK - 1 else [slice(0, 1), slice(1, 2)]):
+                nc.scalar.activation(gate[:, hs, :], pre[:, hs, :], SILU, bias=bias[:, r : r + 1])
+                nc.vector.tensor_tensor(y[:, hs, r, :], lin[:, hs, :], gate[:, hs, :], MULT)
+            nc.sync.dma_start(out_rows[:, r, :, :], y[:, :, r, :])
 
         y_codes = sb.tile([P, NQ], U32, name="y_codes", align_bytes=64)
         y_plane = sb.tile([P, NQ], U8, name="y_plane", align_bytes=64)
         y_bf = [sb.tile([P, HALF, PACK], BF16, name="y_bf%d" % h, align_bytes=64) for h in range(2)]
-        nc.vector.tensor_copy(*interleave_views(y_bf[0][:], y[:, :, 0:HALF]))
-        nc.scalar.copy(*interleave_views(y_bf[1][:], y[:, :, HALF:NQ]))
+        nc.scalar.copy(*interleave_views(y_bf[0][:], y[:, 0, :, :]))
+        nc.vector.tensor_copy(*interleave_views(y_bf[1][:], y[:, 1, :, :]))
         words_out = out_1[0].rearrange("p q b -> p (q b)").bitcast(I32)
-        for h in range(2):
+        for h in (1, 0):
             cols = slice(h * HALF, (h + 1) * HALF)
             nc.vector.quantize_mx(out=y_codes[:, cols].bitcast(FP8X4), scales=y_plane[:, cols], in_=y_bf[h][:].rearrange("p w j -> p (w j)"))
             nc.sync.dma_start(words_out[:, cols], y_codes[:, cols].bitcast(I32))

@@ -24,7 +24,6 @@ HALF = NQ // 2
 BIAS_ROW = P - 1
 SCALE_ROW = 96
 SHARE = 96
-WARM_PASSES = 3
 
 
 def interleave_views(dst, src):
@@ -52,7 +51,6 @@ def tile_attend_plh_bswiglu_topk_kernel(tc, qT, k_words, k_scales, c_words, c_sc
 
         nc.vector.memset(ks_pool[0:SCALE_ROW, :].bitcast(I32), 0)
         nc.vector.memset(cs_pool[0:SCALE_ROW, :].bitcast(I32), 0)
-        nc.vector.memset(nb_pool[0:BIAS_ROW, :], 0.0)
 
         nc.sync.dma_start(offsets[:], offs)
         nc.sync.dma_start(ks_pool[SCALE_ROW:P, :].bitcast(I32), k_scales.rearrange("o f t -> f o t").bitcast(I32))
@@ -65,6 +63,7 @@ def tile_attend_plh_bswiglu_topk_kernel(tc, qT, k_words, k_scales, c_words, c_sc
 
         ident = sb.tile([P, P], F32, name="ident")
         make_identity(nc, ident[:])
+        nc.gpsimd.memset(nb_pool[0:BIAS_ROW, :], 0.0)
 
         def gather_scales(name, pool, tag):
             picked = sb.tile([P, N], U8, name=name + "_picked", tag=tag, align_bytes=64)
@@ -114,17 +113,6 @@ def tile_attend_plh_bswiglu_topk_kernel(tc, qT, k_words, k_scales, c_words, c_sc
         q0_bf = sb.tile([P, NQ, PACK], BF16, name="q0_bf", align_bytes=64)
         nc.scalar.copy(*interleave_views(q0_bf[:], q0_raw[:]))
         nc.vector.quantize_mx(out=q_codes[0][:].bitcast(FP8X4), scales=q_planes[0][:], in_=q0_bf[:].rearrange("p w j -> p (w j)"))
-        warm_bank = psum.tile([P, NQ], F32, name="warm_bank", tag="z2")
-        for i in range(WARM_PASSES):
-            nc.tensor.matmul_mx(
-                out=warm_bank[:],
-                lhsT=kw_pool[:, 0 : P // 2].bitcast(FP4X4),
-                lhsT_scale=ks_pool[:, 0:P],
-                rhs=q_codes[0][:].bitcast(FP8X4),
-                rhs_scale=q_planes[0][:],
-                start=True,
-                stop=True,
-            )
         k_halves = gather_words("kw", kw_pool)
         k_codes = [deal_words("kw", k_halves, 0, 0, PACK)]
         c_halves = gather_words("cw", cw_pool)

@@ -21,9 +21,12 @@ P = 128
 PACK = 4
 PASSES = 2
 HALF = NQ // 2
+CHUNK = 128
+BANK = 512
 BIAS_ROW = P - 1
 SCALE_ROW = 96
-SHARE = 96
+GATE, LIN = 0, 1
+SCALAR_SHARE = 320
 
 
 def interleave_views(dst, src):
@@ -38,144 +41,129 @@ def tile_attend_plh_bswiglu_topk_kernel(tc, qT, k_words, k_scales, c_words, c_sc
 
         offsets = sb.tile([P, N // 16], U16, name="offsets")
         nb_pool = sb.tile([P, T], F32, name="nb_pool")
-        kw_pool = sb.tile([P, T], I32, name="kw_pool", align_bytes=64)
-        cw_pool = sb.tile([P, T], I32, name="cw_pool")
-        ks_pool = sb.tile([P, T], U8, name="ks_pool", align_bytes=64)
-        cs_pool = sb.tile([P, T], U8, name="cs_pool", tag="late0", align_bytes=64)
-        q0_raw = sb.tile([P, PACK, NQ], F32, name="q0_raw")
+        k_pool = sb.tile([P, T], I32, name="k_pool", tag="after_k", align_bytes=64)
+        scale_pools = [sb.tile([P, T], U8, name="scale_pool%d" % t) for t in range(2)]
+        q_raw = [sb.tile([P, PACK, NQ], F32, name="q_raw%d" % o) for o in range(PASSES)]
 
         warm_in = sb.tile([P, 1], F32, name="warm_in")
         warm_out = sb.tile([P, 1], F32, name="warm_out")
         nc.gpsimd.memset(warm_in[:], 0.0)
         nc.scalar.activation(warm_out[:], warm_in[:], SILU)
 
-        nc.vector.memset(ks_pool[0:SCALE_ROW, :].bitcast(I32), 0)
-        nc.vector.memset(cs_pool[0:SCALE_ROW, :].bitcast(I32), 0)
+        for pool in scale_pools:
+            nc.gpsimd.memset(pool[0:SCALE_ROW, :].bitcast(I32), 0)
+        nc.gpsimd.memset(nb_pool[0:BIAS_ROW, :].bitcast(I32), 0)
 
-        nc.sync.dma_start(offsets[:], offs)
-        nc.sync.dma_start(ks_pool[SCALE_ROW:P, :].bitcast(I32), k_scales.rearrange("o f t -> f o t").bitcast(I32))
-        nc.sync.dma_start(cs_pool[SCALE_ROW:P, :].bitcast(I32), c_scales.rearrange("o f t -> f o t").bitcast(I32))
-        nc.sync.dma_start(nb_pool[BIAS_ROW:P, :], nb[0:1, :])
         q_rows = qT[0].rearrange("(o p j) w -> o p j w", o=PASSES, j=PACK)
-        nc.sync.dma_start(q0_raw[:], q_rows[0])
-        for pool, words in ((kw_pool, k_words), (cw_pool, c_words)):
-            nc.sync.dma_start(pool[:], words[0].rearrange("p t b -> p (t b)").bitcast(I32))
+        nc.sync.dma_start(offsets[:], offs)
+        for pool, scales, queue in zip(scale_pools, (k_scales, c_scales), (nc.sync, nc.sync)):
+            queue.dma_start(pool[SCALE_ROW:P, :].bitcast(I32), scales.rearrange("o f t -> f o t").bitcast(I32))
+        nc.sync.dma_start(nb_pool[BIAS_ROW:P, :], nb[0:1, :])
+        nc.sync.dma_start(q_raw[0][:], q_rows[0])
+        nc.sync.dma_start(k_pool[:], k_words[0].rearrange("p t b -> p (t b)").bitcast(I32))
+        nc.sync.dma_start(q_raw[1][:], q_rows[1])
 
+        planes = sb.tile([P, PASSES, 2, N], U8, name="planes", align_bytes=64)
+        nc.gpsimd.memset(planes[:].bitcast(I32), 0)
         ident = sb.tile([P, P], F32, name="ident")
         make_identity(nc, ident[:])
-        nc.gpsimd.memset(nb_pool[0:BIAS_ROW, :], 0.0)
 
-        def gather_scales(name, pool, tag):
-            picked = sb.tile([P, N], U8, name=name + "_picked", tag=tag, align_bytes=64)
-            nc.vector.tensor_copy(picked[:], pool[:].indirect(offsets[:]))
-            return picked
+        picked_scales = [sb.tile([P, N], U8, name="picked_scales%d" % t, tag=("after_deal" if t == LIN else "")) for t in range(2)]
+        dealt = sb.tile([P, 2, N], U8, name="dealt")
+        for t in range(2):
+            nc.vector.tensor_copy(picked_scales[t][:], scale_pools[t][:].indirect(offsets[:]))
+        for t in range(2):
+            nc.vector.tensor_copy(dealt[:, t, :].rearrange("p (r s) -> p r s", r=PACK), picked_scales[t][:].rearrange("p (s r) -> p r s", r=PACK))
 
-        def place_scales(name, picked):
-            planes = sb.tile([P, PASSES, N], U8, name=name + "_planes", align_bytes=64)
-            nc.gpsimd.memset(planes[:].bitcast(I32), 0)
-            dealt = sb.tile([P, N], U8, name=name + "_dealt")
-            nc.vector.tensor_copy(dealt[:].rearrange("p (r s) -> p r s", r=PACK), picked[:].rearrange("p (s r) -> p r s", r=PACK))
-            for quad in range(4):
-                first = SCALE_ROW + 8 * quad
-                nc.scalar.dma_start(planes[32 * quad : 32 * quad + 4, :, :].bitcast(I32), dealt[first : first + 8, :].bitcast(I32))
-            return planes
+        def place_scales(o):
+            for i in range(4):
+                nc.sync.dma_start(
+                    planes[i:P:32, o].rearrange("p t n -> p (t n)").bitcast(I32),
+                    dealt[SCALE_ROW + 2 * i + o : P : 8].rearrange("p t n -> p (t n)").bitcast(I32),
+                )
 
-        ks_picked = gather_scales("ks", ks_pool, "ks_picked")
-        cs_picked = gather_scales("cs", cs_pool, "late1")
-        k_planes = place_scales("ks", ks_picked)
+        place_scales(0)
+        c_pool = sb.tile([P, T], I32, name="c_pool", tag="after_deal")
+        nc.sync.dma_start(c_pool[:], c_words[0].rearrange("p t b -> p (t b)").bitcast(I32))
+        place_scales(1)
         nb_picked = sb.tile([P, N], F32, name="nb_picked")
         nc.vector.tensor_copy(nb_picked[:], nb_pool[:].indirect(offsets[:]))
-        c_planes = place_scales("cs", cs_picked)
 
-        q1_raw = [sb.tile([P, PACK, HALF], F32, name="q1_raw%d" % h, tag="late%d" % h, align_bytes=64) for h in range(2)]
-        for h in range(2):
-            nc.sync.dma_start(q1_raw[h][:], q_rows[1][:, :, h * HALF : (h + 1) * HALF])
-
-        nb_turned = psum.tile([P, PACK, P], F32, name="nb_turned", tag="z3")
+        gate_banks = [psum.tile([P, NQ], F32, name="gate%d" % r) for r in range(PACK)]
+        lin_banks = [psum.tile([P, NQ], F32, name="lin%d" % c) for c in range(4)]
+        nb_turned = lin_banks[3][:].rearrange("p (r s) -> p r s", r=PACK)
         for r in range(PACK):
             nc.tensor.transpose(nb_turned[:, r, :], nb_picked[:, r:N:PACK], ident[:])
         bias = sb.tile([P, PACK], F32, name="bias")
         nc.scalar.copy(bias[:], nb_turned[:, :, BIAS_ROW])
 
-        def gather_words(name, pool):
-            picked = sb.tile([P, N], U32, name=name + "_picked")
+        q_bf = [sb.tile([P, NQ, PACK], BF16, name="q_bf%d" % o, align_bytes=64) for o in range(PASSES)]
+        q_codes = [sb.tile([P, NQ], U32, name="q_codes%d" % o, tag=("" if o else "after_k"), align_bytes=64) for o in range(PASSES)]
+        q_planes = [sb.tile([P, NQ], U8, name="q_plane%d" % o, align_bytes=64) for o in range(PASSES)]
+
+        def round_queries(engine_copy, o, cols):
+            engine_copy(*interleave_views(q_bf[o][:, cols, :], q_raw[o][:, :, cols]))
+
+        def quantise_queries(o):
+            nc.vector.quantize_mx(out=q_codes[o][:].bitcast(FP8X4), scales=q_planes[o][:], in_=q_bf[o][:].rearrange("p w j -> p (w j)"))
+
+        def gather_words(name, pool, tag):
+            picked = sb.tile([P, N], U32, name=name + "_picked", tag=tag)
             nc.vector.tensor_copy(picked[:], pool[:].bitcast(U32).indirect(offsets[:]))
             return picked[:].bitcast(U16).rearrange("p (s r o) -> p o s r", r=PACK, o=PASSES)
 
-        def deal_words(name, halves, o, first, count, tag=""):
-            codes = sb.tile([P, count, 2 * P], U8, name="%s_codes%d_%d" % (name, o, first), tag=tag, align_bytes=64)
-            nc.vector.tensor_copy(codes[:].bitcast(U16).rearrange("p r s -> p s r"), halves[:, o, :, first : first + count])
-            return [codes[:, i, :] for i in range(count)]
+        def deal_words(codes, halves, passes, tiles):
+            nc.vector.tensor_copy(codes[:].bitcast(U16).rearrange("p o r s -> p o s r")[:, passes, :, tiles], halves[:, passes, :, tiles])
 
-        q_codes = [sb.tile([P, NQ], U32, name="q_codes%d" % o, align_bytes=64) for o in range(PASSES)]
-        q_planes = [sb.tile([P, NQ], U8, name="q_plane%d" % o, align_bytes=64) for o in range(PASSES)]
+        w_codes = [sb.tile([P, PASSES, PACK, 2 * P], U8, name="w_codes%d" % t, align_bytes=64) for t in range(2)]
+        round_queries(nc.scalar.copy, 0, slice(0, NQ))
+        k_halves = gather_words("k", k_pool, "")
+        deal_words(w_codes[GATE], k_halves, slice(0, 1), slice(0, PACK))
+        quantise_queries(0)
+        deal_words(w_codes[GATE], k_halves, slice(1, 2), slice(0, PACK))
+        round_queries(nc.scalar.copy, 1, slice(0, SCALAR_SHARE))
+        round_queries(nc.vector.tensor_copy, 1, slice(SCALAR_SHARE, NQ))
+        quantise_queries(1)
 
-        q0_bf = sb.tile([P, NQ, PACK], BF16, name="q0_bf", align_bytes=64)
-        nc.scalar.copy(*interleave_views(q0_bf[:], q0_raw[:]))
-        nc.vector.quantize_mx(out=q_codes[0][:].bitcast(FP8X4), scales=q_planes[0][:], in_=q0_bf[:].rearrange("p w j -> p (w j)"))
-        k_halves = gather_words("kw", kw_pool)
-        k_codes = [deal_words("kw", k_halves, 0, 0, PACK)]
-        c_halves = gather_words("cw", cw_pool)
-        c_codes = [deal_words("cw", c_halves, 0, 0, 2)]
-        k_codes.append(deal_words("kw", k_halves, 1, 0, 2))
-
-        q1_bf = [sb.tile([P, HALF, PACK], BF16, name="q1_bf%d" % h, tag="q1_bf%d" % h, align_bytes=64) for h in range(2)]
-        nc.scalar.copy(*interleave_views(q1_bf[0][:], q1_raw[0][:]))
-        nc.scalar.copy(*interleave_views(q1_bf[1][:, 0:SHARE, :], q1_raw[1][:, :, 0:SHARE]))
-        nc.vector.tensor_copy(*interleave_views(q1_bf[1][:, SHARE:HALF, :], q1_raw[1][:, :, SHARE:HALF]))
-        for h in range(2):
-            cols = slice(h * HALF, (h + 1) * HALF)
-            nc.vector.quantize_mx(out=q_codes[1][:, cols].bitcast(FP8X4), scales=q_planes[1][:, cols], in_=q1_bf[h][:].rearrange("p w j -> p (w j)"))
-        c_codes.append(deal_words("cw", c_halves, 1, 0, 2, "late1"))
-        k_codes[1].extend(deal_words("kw", k_halves, 1, 2, 2, "q1_bf0"))
-        c_late = sb.tile([P, PASSES, 2, 2 * P], U8, name="cw_codes_late", tag="q1_bf1", align_bytes=64)
-        nc.vector.tensor_copy(c_late[:].bitcast(U16).rearrange("p o r s -> p s r o"), c_halves[:, :, :, 2:PACK].rearrange("p o s r -> p s r o"))
-        for o in range(PASSES):
-            c_codes[o].extend([c_late[:, o, i, :] for i in range(2)])
-
-        gate_banks = [psum.tile([P, NQ], F32, name="gate%d" % r, tag="a%d" % r) for r in range(PACK)]
-        lin_banks = [psum.tile([P, NQ], F32, name="lin%d" % r, tag="z%d" % r) for r in range(PACK)]
-
-        def mx_pass(bank, codes, planes, o, r):
+        def mx_pass(out, t, o, r, cols):
             nc.tensor.matmul_mx(
-                out=bank[:],
-                lhsT=codes[o][r].bitcast(FP4X4),
-                lhsT_scale=planes[:, o, P * r : P * (r + 1)],
-                rhs=q_codes[o][:].bitcast(FP8X4),
-                rhs_scale=q_planes[o][:],
+                out=out,
+                lhsT=w_codes[t][:, o, r, :].bitcast(FP4X4),
+                lhsT_scale=planes[:, o, t, P * r : P * (r + 1)],
+                rhs=q_codes[o][:, cols].bitcast(FP8X4),
+                rhs_scale=q_planes[o][:, cols],
                 start=(o == 0),
                 stop=(o == PASSES - 1),
             )
 
+        for o in range(PASSES):
+            for r in range(PACK):
+                mx_pass(gate_banks[r][:], GATE, o, r, slice(0, NQ))
+        gates = sb.tile([P, PACK, NQ], F32, name="gates")
         for r in range(PACK):
-            mx_pass(gate_banks[r], k_codes, k_planes, 0, r)
-        for r in range(2):
-            mx_pass(lin_banks[r], c_codes, c_planes, 0, r)
+            nc.scalar.activation(gates[:, r, :], gate_banks[r][:], SILU, bias=bias[:, r : r + 1])
 
-        y = sb.tile([P, 2, PACK, HALF], F32, name="y")
-        out_rows = out_0.rearrange("(p r) (h q) -> p r h q", r=PACK, h=2)
-        mx_pass(gate_banks[0], k_codes, k_planes, 1, 0)
-        for r in range(PACK):
-            if r + 1 < PACK:
-                mx_pass(gate_banks[r + 1], k_codes, k_planes, 1, r + 1)
-            for o in range(1 if r < 2 else 0, PASSES):
-                mx_pass(lin_banks[r], c_codes, c_planes, o, r)
-            gates = sb.tile([P, NQ], F32, name="gates%d" % r)
-            lin = lin_banks[r][:].rearrange("p (h q) -> p h q", h=2)
-            gate = gates[:].rearrange("p (h q) -> p h q", h=2)
-            pre = gate_banks[r][:].rearrange("p (h q) -> p h q", h=2)
-            for hs in ([slice(0, 2)] if r < PACK - 1 else [slice(0, 1), slice(1, 2)]):
-                nc.scalar.activation(gate[:, hs, :], pre[:, hs, :], SILU, bias=bias[:, r : r + 1])
-                nc.vector.tensor_tensor(y[:, hs, r, :], lin[:, hs, :], gate[:, hs, :], MULT)
-            nc.sync.dma_start(out_rows[:, r, :, :], y[:, :, r, :])
+        c_halves = gather_words("c", c_pool, "")
+        deal_words(w_codes[LIN], c_halves, slice(0, 2), slice(0, 1))
+        deal_words(w_codes[LIN], c_halves, slice(0, 2), slice(1, PACK))
 
+        out_rows = out_0.rearrange("(p r) q -> p r q", r=PACK)
+        words_out = out_1[0].rearrange("p q b -> p (q b)").bitcast(I32)
         y_codes = sb.tile([P, NQ], U32, name="y_codes", align_bytes=64)
         y_plane = sb.tile([P, NQ], U8, name="y_plane", align_bytes=64)
+        y = sb.tile([P, PACK, NQ], F32, name="y")
         y_bf = [sb.tile([P, HALF, PACK], BF16, name="y_bf%d" % h, align_bytes=64) for h in range(2)]
-        nc.scalar.copy(*interleave_views(y_bf[0][:], y[:, 0, :, :]))
-        nc.vector.tensor_copy(*interleave_views(y_bf[1][:], y[:, 1, :, :]))
-        words_out = out_1[0].rearrange("p q b -> p (q b)").bitcast(I32)
-        for h in (1, 0):
+
+        for r in range(PACK):
+            for o in range(PASSES):
+                mx_pass(lin_banks[r][:], LIN, o, r, slice(0, NQ))
+            for cols in ([slice(0, NQ)] if r < PACK - 1 else [slice(0, HALF), slice(HALF, NQ)]):
+                nc.vector.tensor_tensor(y[:, r, cols], lin_banks[r][:, cols], gates[:, r, cols], MULT)
+            nc.sync.dma_start(out_rows[:, r, :], y[:, r, :])
+        for c, engine_copy in enumerate((nc.scalar.copy, nc.vector.tensor_copy) * 2):
+            within = slice((c % 2) * CHUNK, (c % 2 + 1) * CHUNK)
+            engine_copy(*interleave_views(y_bf[c // 2][:, within, :], y[:, :, c * CHUNK : (c + 1) * CHUNK]))
+        for h in range(2):
             cols = slice(h * HALF, (h + 1) * HALF)
             nc.vector.quantize_mx(out=y_codes[:, cols].bitcast(FP8X4), scales=y_plane[:, cols], in_=y_bf[h][:].rearrange("p w j -> p (w j)"))
             nc.sync.dma_start(words_out[:, cols], y_codes[:, cols].bitcast(I32))

@@ -26,7 +26,7 @@ BANK = 512
 BIAS_ROW = P - 1
 SCALE_ROW = 96
 GATE, LIN = 0, 1
-SCALAR_SHARE = 320
+SCALAR_SHARE = 48
 
 
 def interleave_views(dst, src):
@@ -90,8 +90,8 @@ def tile_attend_plh_bswiglu_topk_kernel(tc, qT, k_words, k_scales, c_words, c_sc
         nc.vector.tensor_copy(nb_picked[:], nb_pool[:].indirect(offsets[:]))
 
         gate_banks = [psum.tile([P, NQ], F32, name="gate%d" % r) for r in range(PACK)]
-        lin_banks = [psum.tile([P, NQ], F32, name="lin%d" % c) for c in range(4)]
-        nb_turned = lin_banks[3][:].rearrange("p (r s) -> p r s", r=PACK)
+        lin_banks = [psum.tile([P, PACK, CHUNK], F32, name="lin%d" % c) for c in range(4)]
+        nb_turned = lin_banks[3]
         for r in range(PACK):
             nc.tensor.transpose(nb_turned[:, r, :], nb_picked[:, r:N:PACK], ident[:])
         bias = sb.tile([P, PACK], F32, name="bias")
@@ -104,8 +104,8 @@ def tile_attend_plh_bswiglu_topk_kernel(tc, qT, k_words, k_scales, c_words, c_sc
         def round_queries(engine_copy, o, cols):
             engine_copy(*interleave_views(q_bf[o][:, cols, :], q_raw[o][:, :, cols]))
 
-        def quantise_queries(o):
-            nc.vector.quantize_mx(out=q_codes[o][:].bitcast(FP8X4), scales=q_planes[o][:], in_=q_bf[o][:].rearrange("p w j -> p (w j)"))
+        def quantise_queries(o, cols):
+            nc.vector.quantize_mx(out=q_codes[o][:, cols].bitcast(FP8X4), scales=q_planes[o][:, cols], in_=q_bf[o][:, cols, :].rearrange("p w j -> p (w j)"))
 
         def gather_words(name, pool, tag):
             picked = sb.tile([P, N], U32, name=name + "_picked", tag=tag)
@@ -115,58 +115,76 @@ def tile_attend_plh_bswiglu_topk_kernel(tc, qT, k_words, k_scales, c_words, c_sc
         def deal_words(codes, halves, passes, tiles):
             nc.vector.tensor_copy(codes[:].bitcast(U16).rearrange("p o r s -> p o s r")[:, passes, :, tiles], halves[:, passes, :, tiles])
 
-        w_codes = [sb.tile([P, PASSES, PACK, 2 * P], U8, name="w_codes%d" % t, align_bytes=64) for t in range(2)]
+        w_codes = [sb.tile([P, PASSES, PACK, 2 * P], U8, name="w_codes%d" % t, tag=("after_gate" if t == GATE else ""), align_bytes=64) for t in range(2)]
         round_queries(nc.scalar.copy, 0, slice(0, NQ))
         k_halves = gather_words("k", k_pool, "")
         deal_words(w_codes[GATE], k_halves, slice(0, 1), slice(0, PACK))
-        quantise_queries(0)
+        quantise_queries(0, slice(0, NQ))
         deal_words(w_codes[GATE], k_halves, slice(1, 2), slice(0, PACK))
-        round_queries(nc.scalar.copy, 1, slice(0, SCALAR_SHARE))
-        round_queries(nc.vector.tensor_copy, 1, slice(SCALAR_SHARE, NQ))
-        quantise_queries(1)
+        round_queries(nc.vector.tensor_copy, 1, slice(0, CHUNK))
+        round_queries(nc.scalar.copy, 1, slice(CHUNK, HALF))
+        quantise_queries(1, slice(0, HALF))
+        round_queries(nc.scalar.copy, 1, slice(HALF, NQ))
+        quantise_queries(1, slice(HALF, NQ))
 
-        def mx_pass(out, t, o, r, cols):
+        def mx_pass(out, t, o, r, cols, first):
             nc.tensor.matmul_mx(
                 out=out,
                 lhsT=w_codes[t][:, o, r, :].bitcast(FP4X4),
                 lhsT_scale=planes[:, o, t, P * r : P * (r + 1)],
                 rhs=q_codes[o][:, cols].bitcast(FP8X4),
                 rhs_scale=q_planes[o][:, cols],
-                start=(o == 0),
-                stop=(o == PASSES - 1),
+                start=first,
+                stop=not first,
             )
 
         for o in range(PASSES):
             for r in range(PACK):
-                mx_pass(gate_banks[r][:], GATE, o, r, slice(0, NQ))
-        gates = sb.tile([P, PACK, NQ], F32, name="gates")
-        for r in range(PACK):
-            nc.scalar.activation(gates[:, r, :], gate_banks[r][:], SILU, bias=bias[:, r : r + 1])
+                mx_pass(gate_banks[r][:], GATE, o, r, slice(0, NQ), o == 0)
+        gates = [sb.tile([P, PACK, HALF], F32, name="gates%d" % h, tag=("after_gate" if h else ""), align_bytes=64) for h in range(2)]
+        for h in range(2):
+            for r in range(PACK):
+                nc.scalar.activation(gates[h][:, r, :], gate_banks[r][:, h * HALF : (h + 1) * HALF], SILU, bias=bias[:, r : r + 1])
 
         c_halves = gather_words("c", c_pool, "")
-        deal_words(w_codes[LIN], c_halves, slice(0, 2), slice(0, 1))
-        deal_words(w_codes[LIN], c_halves, slice(0, 2), slice(1, PACK))
+        deal_words(w_codes[LIN], c_halves, slice(0, 2), slice(0, 2))
+        deal_words(w_codes[LIN], c_halves, slice(0, 2), slice(2, PACK))
 
         out_rows = out_0.rearrange("(p r) q -> p r q", r=PACK)
         words_out = out_1[0].rearrange("p q b -> p (q b)").bitcast(I32)
         y_codes = sb.tile([P, NQ], U32, name="y_codes", align_bytes=64)
         y_plane = sb.tile([P, NQ], U8, name="y_plane", align_bytes=64)
-        y = sb.tile([P, PACK, NQ], F32, name="y")
-        y_bf = [sb.tile([P, HALF, PACK], BF16, name="y_bf%d" % h, align_bytes=64) for h in range(2)]
+        y = [sb.tile([P, PACK, CHUNK], F32, name="y%d" % c) for c in range(4)]
+        y_bf = sb.tile([P, NQ, PACK], BF16, name="y_bf", align_bytes=64)
 
-        for r in range(PACK):
-            for o in range(PASSES):
-                mx_pass(lin_banks[r][:], LIN, o, r, slice(0, NQ))
-            for cols in ([slice(0, NQ)] if r < PACK - 1 else [slice(0, HALF), slice(HALF, NQ)]):
-                nc.vector.tensor_tensor(y[:, r, cols], lin_banks[r][:, cols], gates[:, r, cols], MULT)
-            nc.sync.dma_start(out_rows[:, r, :], y[:, r, :])
-        for c, engine_copy in enumerate((nc.scalar.copy, nc.vector.tensor_copy) * 2):
-            within = slice((c % 2) * CHUNK, (c % 2 + 1) * CHUNK)
-            engine_copy(*interleave_views(y_bf[c // 2][:, within, :], y[:, :, c * CHUNK : (c + 1) * CHUNK]))
-        for h in range(2):
-            cols = slice(h * HALF, (h + 1) * HALF)
-            nc.vector.quantize_mx(out=y_codes[:, cols].bitcast(FP8X4), scales=y_plane[:, cols], in_=y_bf[h][:].rearrange("p w j -> p (w j)"))
+        def gated(c):
+            cols = slice(c * CHUNK, (c + 1) * CHUNK)
+            for r in range(PACK):
+                for o in (1, 0):
+                    mx_pass(lin_banks[c][:, r, :], LIN, o, r, cols, o == 1)
+            nc.vector.tensor_tensor(y[c][:], lin_banks[c][:], gates[c // 2][:, :, (c % 2) * CHUNK : (c % 2 + 1) * CHUNK], MULT)
+            nc.sync.dma_start(out_rows[:, :, cols], y[c][:])
+
+        def round_result(engine_copy, c, first, last):
+            engine_copy(*interleave_views(y_bf[:, c * CHUNK + first : c * CHUNK + last, :], y[c][:, :, first:last]))
+
+        def quantise_result(cols):
+            nc.vector.quantize_mx(out=y_codes[:, cols].bitcast(FP8X4), scales=y_plane[:, cols], in_=y_bf[:, cols, :].rearrange("p w j -> p (w j)"))
+
+        def store_words(cols):
             nc.sync.dma_start(words_out[:, cols], y_codes[:, cols].bitcast(I32))
+
+        for c in range(3):
+            gated(c)
+            round_result(nc.scalar.copy, c, 0, CHUNK)
+        quantise_result(slice(0, HALF))
+        store_words(slice(0, HALF))
+        gated(3)
+        quantise_result(slice(HALF, HALF + CHUNK))
+        round_result(nc.scalar.copy, 3, 0, SCALAR_SHARE)
+        round_result(nc.vector.tensor_copy, 3, SCALAR_SHARE, CHUNK)
+        quantise_result(slice(HALF + CHUNK, NQ))
+        store_words(slice(HALF, NQ))
         for quad in range(4):
             queue = nc.scalar if quad % 2 else nc.sync
             queue.dma_start(out_2[0, 4 * quad : 4 * quad + 4, :].bitcast(I32), y_plane[32 * quad : 32 * quad + 4, :].bitcast(I32))

@@ -40,7 +40,7 @@ def tile_attend_plh_bswiglu_topk_kernel(tc, qT, k_words, k_scales, c_words, c_sc
         psum = ctx.enter_context(tc.psum_pool(name="psum", bufs=1))
 
         offsets = sb.tile([P, N // 16], U16, name="offsets")
-        nb_pool = sb.tile([P, T], F32, name="nb_pool")
+        nb_pool = sb.tile([P, T + 1], F32, name="nb_pool")
         k_pool = sb.tile([P, T], I32, name="k_pool", tag="after_k", align_bytes=64)
         scale_pools = [sb.tile([P, T], U8, name="scale_pool%d" % t) for t in range(2)]
         q_raw = [sb.tile([P, PACK, NQ], F32, name="q_raw%d" % o) for o in range(PASSES)]
@@ -52,13 +52,13 @@ def tile_attend_plh_bswiglu_topk_kernel(tc, qT, k_words, k_scales, c_words, c_sc
 
         for pool in scale_pools:
             nc.gpsimd.memset(pool[0:SCALE_ROW, :].bitcast(I32), 0)
-        nc.gpsimd.memset(nb_pool[0:BIAS_ROW, :].bitcast(I32), 0)
+        nc.vector.memset(nb_pool[0:BIAS_ROW, :].bitcast(I32), 0)
 
         q_rows = qT[0].rearrange("(o p j) w -> o p j w", o=PASSES, j=PACK)
         nc.sync.dma_start(offsets[:], offs)
         for pool, scales, queue in zip(scale_pools, (k_scales, c_scales), (nc.sync, nc.sync)):
             queue.dma_start(pool[SCALE_ROW:P, :].bitcast(I32), scales.rearrange("o f t -> f o t").bitcast(I32))
-        nc.sync.dma_start(nb_pool[BIAS_ROW:P, :], nb[0:1, :])
+        nc.sync.dma_start(nb_pool[BIAS_ROW:P, 0:T], nb[0:1, :])
         nc.sync.dma_start(q_raw[0][:], q_rows[0])
         nc.sync.dma_start(k_pool[:], k_words[0].rearrange("p t b -> p (t b)").bitcast(I32))
         nc.sync.dma_start(q_raw[1][:], q_rows[1])
@@ -87,7 +87,7 @@ def tile_attend_plh_bswiglu_topk_kernel(tc, qT, k_words, k_scales, c_words, c_sc
         nc.sync.dma_start(c_pool[:], c_words[0].rearrange("p t b -> p (t b)").bitcast(I32))
         place_scales(1)
         nb_picked = sb.tile([P, N], F32, name="nb_picked")
-        nc.vector.tensor_copy(nb_picked[:], nb_pool[:].indirect(offsets[:]))
+        nc.vector.tensor_copy(nb_picked[:], nb_pool[:, 0:T].indirect(offsets[:]))
 
         gate_banks = [psum.tile([P, NQ], F32, name="gate%d" % r) for r in range(PACK)]
         lin_banks = [psum.tile([P, PACK, CHUNK], F32, name="lin%d" % c) for c in range(4)]

@@ -55,11 +55,12 @@ def tile_attend_plh_bswiglu_topk_kernel(tc, qT, k_words, k_scales, c_words, c_sc
         nc.vector.memset(nb_pool[0:BIAS_ROW, :].bitcast(I32), 0)
 
         q_rows = qT[0].rearrange("(o p j) w -> o p j w", o=PASSES, j=PACK)
+        nc.scalar.dma_start(q_raw[0][:, 0:1, :], q_rows[0][:, 0:1, :])
         nc.sync.dma_start(offsets[:], offs)
         for pool, scales, queue in zip(scale_pools, (k_scales, c_scales), (nc.sync, nc.sync)):
             queue.dma_start(pool[SCALE_ROW:P, :].bitcast(I32), scales.rearrange("o f t -> f o t").bitcast(I32))
         nc.sync.dma_start(nb_pool[BIAS_ROW:P, 0:T], nb[0:1, :])
-        nc.sync.dma_start(q_raw[0][:], q_rows[0])
+        nc.sync.dma_start(q_raw[0][:, 1:PACK, :], q_rows[0][:, 1:PACK, :])
         nc.sync.dma_start(k_pool[:], k_words[0].rearrange("p t b -> p (t b)").bitcast(I32))
         nc.sync.dma_start(q_raw[1][:], q_rows[1])
 
@@ -75,17 +76,13 @@ def tile_attend_plh_bswiglu_topk_kernel(tc, qT, k_words, k_scales, c_words, c_sc
         for t in range(2):
             nc.vector.tensor_copy(dealt[:, t, :].rearrange("p (r s) -> p r s", r=PACK), picked_scales[t][:].rearrange("p (s r) -> p r s", r=PACK))
 
-        def place_scales(o):
-            for i in range(4):
-                nc.sync.dma_start(
-                    planes[i:P:32, o].rearrange("p t n -> p (t n)").bitcast(I32),
-                    dealt[SCALE_ROW + 2 * i + o : P : 8].rearrange("p t n -> p (t n)").bitcast(I32),
-                )
-
-        place_scales(0)
+        for quad in range(4):
+            nc.sync.dma_start(
+                planes[32 * quad : 32 * quad + 4].rearrange("p o t n -> p o (t n)").bitcast(I32),
+                dealt[SCALE_ROW + 8 * quad : SCALE_ROW + 8 * quad + 8].rearrange("p t n -> p (t n)").bitcast(I32),
+            )
         c_pool = sb.tile([P, T], I32, name="c_pool", tag="after_deal")
         nc.sync.dma_start(c_pool[:], c_words[0].rearrange("p t b -> p (t b)").bitcast(I32))
-        place_scales(1)
         nb_picked = sb.tile([P, N], F32, name="nb_picked")
         nc.vector.tensor_copy(nb_picked[:], nb_pool[:, 0:T].indirect(offsets[:]))
 
@@ -118,9 +115,9 @@ def tile_attend_plh_bswiglu_topk_kernel(tc, qT, k_words, k_scales, c_words, c_sc
         w_codes = [sb.tile([P, PASSES, PACK, 2 * P], U8, name="w_codes%d" % t, tag=("after_gate" if t == GATE else ""), align_bytes=64) for t in range(2)]
         round_queries(nc.scalar.copy, 0, slice(0, NQ))
         k_halves = gather_words("k", k_pool, "")
-        deal_words(w_codes[GATE], k_halves, slice(0, 1), slice(0, PACK))
+        deal_words(w_codes[GATE], k_halves, slice(0, 2), slice(0, 2))
         quantise_queries(0, slice(0, NQ))
-        deal_words(w_codes[GATE], k_halves, slice(1, 2), slice(0, PACK))
+        deal_words(w_codes[GATE], k_halves, slice(0, 2), slice(2, PACK))
         round_queries(nc.vector.tensor_copy, 1, slice(0, CHUNK))
         round_queries(nc.scalar.copy, 1, slice(CHUNK, HALF))
         quantise_queries(1, slice(0, HALF))
@@ -178,13 +175,13 @@ def tile_attend_plh_bswiglu_topk_kernel(tc, qT, k_words, k_scales, c_words, c_sc
             gated(c)
             round_result(nc.scalar.copy, c, 0, CHUNK)
         quantise_result(slice(0, HALF))
-        store_words(slice(0, HALF))
         gated(3)
         quantise_result(slice(HALF, HALF + CHUNK))
+        store_words(slice(0, HALF + CHUNK))
         round_result(nc.scalar.copy, 3, 0, SCALAR_SHARE)
         round_result(nc.vector.tensor_copy, 3, SCALAR_SHARE, CHUNK)
         quantise_result(slice(HALF + CHUNK, NQ))
-        store_words(slice(HALF, NQ))
+        store_words(slice(HALF + CHUNK, NQ))
         for quad in range(4):
             queue = nc.scalar if quad % 2 else nc.sync
             queue.dma_start(out_2[0, 4 * quad : 4 * quad + 4, :].bitcast(I32), y_plane[32 * quad : 32 * quad + 4, :].bitcast(I32))

@@ -16,6 +16,7 @@ FP8X4 = mybir.dt.float8_e4m3fn_x4
 FP4X4 = mybir.dt.float4_e2m1fn_x4
 SILU = mybir.ActivationFunctionType.Silu
 MULT = mybir.AluOpType.mult
+ADD = mybir.AluOpType.add
 
 P = 128
 PACK = 4
@@ -24,7 +25,7 @@ HALF = NQ // 2
 CHUNK = 128
 BANK = 512
 BIAS_ROW = P - 1
-SCALE_ROW = 96
+SCALE_ROWS = (96, 32)
 GATE, LIN = 0, 1
 SCALAR_SHARE = 48
 
@@ -50,39 +51,41 @@ def tile_attend_plh_bswiglu_topk_kernel(tc, qT, k_words, k_scales, c_words, c_sc
         nc.gpsimd.memset(warm_in[:], 0.0)
         nc.scalar.activation(warm_out[:], warm_in[:], SILU)
 
-        for pool in scale_pools:
-            nc.gpsimd.memset(pool[0:SCALE_ROW, :].bitcast(I32), 0)
+        nc.gpsimd.memset(scale_pools[GATE][0:96, :].bitcast(I32), 0)
+        nc.gpsimd.memset(scale_pools[LIN][0:32, :].bitcast(I32), 0)
+        nc.gpsimd.memset(scale_pools[LIN][64:P, :].bitcast(I32), 0)
         nc.vector.memset(nb_pool[0:BIAS_ROW, :].bitcast(I32), 0)
 
         q_rows = qT[0].rearrange("(o p j) w -> o p j w", o=PASSES, j=PACK)
-        nc.scalar.dma_start(q_raw[0][:, 0:1, :], q_rows[0][:, 0:1, :])
         nc.sync.dma_start(offsets[:], offs)
-        for pool, scales, queue in zip(scale_pools, (k_scales, c_scales), (nc.sync, nc.sync)):
-            queue.dma_start(pool[SCALE_ROW:P, :].bitcast(I32), scales.rearrange("o f t -> f o t").bitcast(I32))
+        for pool, scales, row in zip(scale_pools, (k_scales, c_scales), SCALE_ROWS):
+            nc.sync.dma_start(pool[row : row + 32, :].bitcast(I32), scales.rearrange("o f t -> f o t").bitcast(I32))
         nc.sync.dma_start(nb_pool[BIAS_ROW:P, 0:T], nb[0:1, :])
-        nc.sync.dma_start(q_raw[0][:, 1:PACK, :], q_rows[0][:, 1:PACK, :])
+        nc.sync.dma_start(q_raw[0][:], q_rows[0])
         nc.sync.dma_start(k_pool[:], k_words[0].rearrange("p t b -> p (t b)").bitcast(I32))
-        nc.sync.dma_start(q_raw[1][:], q_rows[1])
 
-        planes = sb.tile([P, PASSES, 2, N], U8, name="planes", align_bytes=64)
+        planes = sb.tile([P, 2, PASSES, N], U8, name="planes", align_bytes=64)
         nc.gpsimd.memset(planes[:].bitcast(I32), 0)
         ident = sb.tile([P, P], F32, name="ident")
         make_identity(nc, ident[:])
 
-        picked_scales = [sb.tile([P, N], U8, name="picked_scales%d" % t, tag=("after_deal" if t == LIN else "")) for t in range(2)]
+        picked_scales = [sb.tile([P, N], U8, name="picked_scales%d" % t) for t in range(2)]
         dealt = sb.tile([P, 2, N], U8, name="dealt")
         for t in range(2):
             nc.vector.tensor_copy(picked_scales[t][:], scale_pools[t][:].indirect(offsets[:]))
         for t in range(2):
             nc.vector.tensor_copy(dealt[:, t, :].rearrange("p (r s) -> p r s", r=PACK), picked_scales[t][:].rearrange("p (s r) -> p r s", r=PACK))
 
-        for quad in range(4):
-            nc.sync.dma_start(
-                planes[32 * quad : 32 * quad + 4].rearrange("p o t n -> p o (t n)").bitcast(I32),
-                dealt[SCALE_ROW + 8 * quad : SCALE_ROW + 8 * quad + 8].rearrange("p t n -> p (t n)").bitcast(I32),
-            )
-        c_pool = sb.tile([P, T], I32, name="c_pool", tag="after_deal")
+        def place_scales(t):
+            for quad in (0, 2, 1, 3):
+                first = SCALE_ROWS[t] + 8 * quad
+                nc.sync.dma_start(planes[32 * quad : 32 * quad + 4, t].bitcast(I32), dealt[first : first + 8, t, :].bitcast(I32))
+
+        place_scales(GATE)
+        nc.sync.dma_start(q_raw[1][:], q_rows[1])
+        c_pool = sb.tile([P, T], I32, name="c_pool")
         nc.sync.dma_start(c_pool[:], c_words[0].rearrange("p t b -> p (t b)").bitcast(I32))
+        place_scales(LIN)
         nb_picked = sb.tile([P, N], F32, name="nb_picked")
         nc.vector.tensor_copy(nb_picked[:], nb_pool[:, 0:T].indirect(offsets[:]))
 
@@ -118,17 +121,17 @@ def tile_attend_plh_bswiglu_topk_kernel(tc, qT, k_words, k_scales, c_words, c_sc
         deal_words(w_codes[GATE], k_halves, slice(0, 2), slice(0, 2))
         quantise_queries(0, slice(0, NQ))
         deal_words(w_codes[GATE], k_halves, slice(0, 2), slice(2, PACK))
-        round_queries(nc.vector.tensor_copy, 1, slice(0, CHUNK))
-        round_queries(nc.scalar.copy, 1, slice(CHUNK, HALF))
+        round_queries(nc.vector.tensor_copy, 1, slice(0, HALF))
+        round_queries(nc.vector.tensor_copy, 1, slice(HALF, HALF + 64))
+        round_queries(nc.scalar.copy, 1, slice(HALF + 64, NQ))
         quantise_queries(1, slice(0, HALF))
-        round_queries(nc.scalar.copy, 1, slice(HALF, NQ))
         quantise_queries(1, slice(HALF, NQ))
 
         def mx_pass(out, t, o, r, cols, first):
             nc.tensor.matmul_mx(
                 out=out,
                 lhsT=w_codes[t][:, o, r, :].bitcast(FP4X4),
-                lhsT_scale=planes[:, o, t, P * r : P * (r + 1)],
+                lhsT_scale=planes[:, t, o, P * r : P * (r + 1)],
                 rhs=q_codes[o][:, cols].bitcast(FP8X4),
                 rhs_scale=q_planes[o][:, cols],
                 start=first,
@@ -154,12 +157,16 @@ def tile_attend_plh_bswiglu_topk_kernel(tc, qT, k_words, k_scales, c_words, c_sc
         y = [sb.tile([P, PACK, CHUNK], F32, name="y%d" % c) for c in range(4)]
         y_bf = sb.tile([P, NQ, PACK], BF16, name="y_bf", align_bytes=64)
 
+        pair_banks = [bank[:] for bank in lin_banks] + [bank[:].rearrange("p (r s) -> p r s", r=PACK) for bank in gate_banks]
+
         def gated(c):
             cols = slice(c * CHUNK, (c + 1) * CHUNK)
-            for r in range(PACK):
-                for o in (1, 0):
-                    mx_pass(lin_banks[c][:, r, :], LIN, o, r, cols, o == 1)
-            nc.vector.tensor_tensor(y[c][:], lin_banks[c][:], gates[c // 2][:, :, (c % 2) * CHUNK : (c % 2 + 1) * CHUNK], MULT)
+            for first, last in ((0, 2), (2, PACK)):
+                bank = pair_banks[2 * c + first // 2]
+                for r in range(first, last):
+                    for o in (1, 0):
+                        mx_pass(bank[:, r, :], LIN, o, r, cols, o == 1)
+                nc.vector.tensor_tensor(y[c][:, first:last, :], bank[:, first:last, :], gates[c // 2][:, first:last, (c % 2) * CHUNK : (c % 2 + 1) * CHUNK], MULT)
             nc.sync.dma_start(out_rows[:, :, cols], y[c][:])
 
         def round_result(engine_copy, c, first, last):
@@ -171,7 +178,9 @@ def tile_attend_plh_bswiglu_topk_kernel(tc, qT, k_words, k_scales, c_words, c_sc
         def store_words(cols):
             nc.sync.dma_start(words_out[:, cols], y_codes[:, cols].bitcast(I32))
 
-        for c in range(3):
+        gated(0)
+        nc.gpsimd.tensor_scalar(y_bf[:, 0:CHUNK, :], y[0][:].rearrange("p t c -> p c t"), 1.0, 0.0, MULT, ADD)
+        for c in (1, 2):
             gated(c)
             round_result(nc.scalar.copy, c, 0, CHUNK)
         quantise_result(slice(0, HALF))

@@ -41,10 +41,12 @@ def tile_attend_plh_bswiglu_topk_kernel(tc, qT, k_words, k_scales, c_words, c_sc
         psum = ctx.enter_context(tc.psum_pool(name="psum", bufs=1))
 
         offsets = sb.tile([P, N // 16], U16, name="offsets")
-        nb_pool = sb.tile([P, T + 1], F32, name="nb_pool")
+        nb_pool = sb.tile([P, T], F32, name="nb_pool")
         k_pool = sb.tile([P, T], I32, name="k_pool", tag="after_k", align_bytes=64)
         scale_pools = [sb.tile([P, T], U8, name="scale_pool%d" % t) for t in range(2)]
-        q_raw = [sb.tile([P, PACK, NQ], F32, name="q_raw%d" % o) for o in range(PASSES)]
+        q_first = sb.tile([P, PACK, NQ], F32, name="q_first")
+        q_early = sb.tile([P, PACK, HALF], F32, name="q_early")
+        q_late = sb.tile([P, PACK, HALF], F32, name="q_late")
 
         warm_in = sb.tile([P, 1], F32, name="warm_in")
         warm_out = sb.tile([P, 1], F32, name="warm_out")
@@ -54,14 +56,15 @@ def tile_attend_plh_bswiglu_topk_kernel(tc, qT, k_words, k_scales, c_words, c_sc
         nc.gpsimd.memset(scale_pools[GATE][0:96, :].bitcast(I32), 0)
         nc.gpsimd.memset(scale_pools[LIN][0:32, :].bitcast(I32), 0)
         nc.gpsimd.memset(scale_pools[LIN][64:P, :].bitcast(I32), 0)
-        nc.vector.memset(nb_pool[0:BIAS_ROW, :].bitcast(I32), 0)
+        for cols in (slice(0, T - 1), slice(T - 1, T)):
+            nc.vector.memset(nb_pool[0:BIAS_ROW, cols].bitcast(I32), 0)
 
         q_rows = qT[0].rearrange("(o p j) w -> o p j w", o=PASSES, j=PACK)
         nc.sync.dma_start(offsets[:], offs)
         for pool, scales, row in zip(scale_pools, (k_scales, c_scales), SCALE_ROWS):
             nc.sync.dma_start(pool[row : row + 32, :].bitcast(I32), scales.rearrange("o f t -> f o t").bitcast(I32))
-        nc.sync.dma_start(nb_pool[BIAS_ROW:P, 0:T], nb[0:1, :])
-        nc.sync.dma_start(q_raw[0][:], q_rows[0])
+        nc.sync.dma_start(nb_pool[BIAS_ROW:P, :], nb[0:1, :])
+        nc.sync.dma_start(q_first[:], q_rows[0])
         nc.sync.dma_start(k_pool[:], k_words[0].rearrange("p t b -> p (t b)").bitcast(I32))
 
         planes = sb.tile([P, 2, PASSES, N], U8, name="planes", align_bytes=64)
@@ -82,12 +85,13 @@ def tile_attend_plh_bswiglu_topk_kernel(tc, qT, k_words, k_scales, c_words, c_sc
                 nc.sync.dma_start(planes[32 * quad : 32 * quad + 4, t].bitcast(I32), dealt[first : first + 8, t, :].bitcast(I32))
 
         place_scales(GATE)
-        nc.sync.dma_start(q_raw[1][:], q_rows[1])
+        nc.sync.dma_start(q_early[:], q_rows[1][:, :, 0:HALF])
+        nc.sync.dma_start(q_late[:], q_rows[1][:, :, HALF:NQ])
         c_pool = sb.tile([P, T], I32, name="c_pool")
         nc.sync.dma_start(c_pool[:], c_words[0].rearrange("p t b -> p (t b)").bitcast(I32))
         place_scales(LIN)
         nb_picked = sb.tile([P, N], F32, name="nb_picked")
-        nc.vector.tensor_copy(nb_picked[:], nb_pool[:, 0:T].indirect(offsets[:]))
+        nc.vector.tensor_copy(nb_picked[:], nb_pool[:].indirect(offsets[:]))
 
         gate_banks = [psum.tile([P, NQ], F32, name="gate%d" % r) for r in range(PACK)]
         lin_banks = [psum.tile([P, PACK, CHUNK], F32, name="lin%d" % c) for c in range(4)]
@@ -101,8 +105,8 @@ def tile_attend_plh_bswiglu_topk_kernel(tc, qT, k_words, k_scales, c_words, c_sc
         q_codes = [sb.tile([P, NQ], U32, name="q_codes%d" % o, tag=("" if o else "after_k"), align_bytes=64) for o in range(PASSES)]
         q_planes = [sb.tile([P, NQ], U8, name="q_plane%d" % o, align_bytes=64) for o in range(PASSES)]
 
-        def round_queries(engine_copy, o, cols):
-            engine_copy(*interleave_views(q_bf[o][:, cols, :], q_raw[o][:, :, cols]))
+        def round_queries(engine_copy, o, cols, raw):
+            engine_copy(*interleave_views(q_bf[o][:, cols, :], raw[:]))
 
         def quantise_queries(o, cols):
             nc.vector.quantize_mx(out=q_codes[o][:, cols].bitcast(FP8X4), scales=q_planes[o][:, cols], in_=q_bf[o][:, cols, :].rearrange("p w j -> p (w j)"))
@@ -116,14 +120,13 @@ def tile_attend_plh_bswiglu_topk_kernel(tc, qT, k_words, k_scales, c_words, c_sc
             nc.vector.tensor_copy(codes[:].bitcast(U16).rearrange("p o r s -> p o s r")[:, passes, :, tiles], halves[:, passes, :, tiles])
 
         w_codes = [sb.tile([P, PASSES, PACK, 2 * P], U8, name="w_codes%d" % t, tag=("after_gate" if t == GATE else ""), align_bytes=64) for t in range(2)]
-        round_queries(nc.scalar.copy, 0, slice(0, NQ))
+        round_queries(nc.scalar.copy, 0, slice(0, NQ), q_first)
         k_halves = gather_words("k", k_pool, "")
         deal_words(w_codes[GATE], k_halves, slice(0, 2), slice(0, 2))
         quantise_queries(0, slice(0, NQ))
         deal_words(w_codes[GATE], k_halves, slice(0, 2), slice(2, PACK))
-        round_queries(nc.vector.tensor_copy, 1, slice(0, HALF))
-        round_queries(nc.vector.tensor_copy, 1, slice(HALF, HALF + 64))
-        round_queries(nc.scalar.copy, 1, slice(HALF + 64, NQ))
+        round_queries(nc.scalar.copy, 1, slice(0, HALF), q_early)
+        round_queries(nc.vector.tensor_copy, 1, slice(HALF, NQ), q_late)
         quantise_queries(1, slice(0, HALF))
         quantise_queries(1, slice(HALF, NQ))
 
@@ -154,20 +157,27 @@ def tile_attend_plh_bswiglu_topk_kernel(tc, qT, k_words, k_scales, c_words, c_sc
         words_out = out_1[0].rearrange("p q b -> p (q b)").bitcast(I32)
         y_codes = sb.tile([P, NQ], U32, name="y_codes", align_bytes=64)
         y_plane = sb.tile([P, NQ], U8, name="y_plane", align_bytes=64)
-        y = [sb.tile([P, PACK, CHUNK], F32, name="y%d" % c) for c in range(4)]
+        y_low = sb.tile([P, PACK, HALF], F32, name="y_low")
+        y = [y_low[:, :, 0:CHUNK], y_low[:, :, CHUNK:HALF]] + [sb.tile([P, PACK, CHUNK], F32, name="y%d" % c)[:] for c in (2, 3)]
         y_bf = sb.tile([P, NQ, PACK], BF16, name="y_bf", align_bytes=64)
 
-        pair_banks = [bank[:] for bank in lin_banks] + [bank[:].rearrange("p (r s) -> p r s", r=PACK) for bank in gate_banks]
+        def layer_sum(out, r, c):
+            for o in (1, 0):
+                mx_pass(out, LIN, o, r, slice(c * CHUNK, (c + 1) * CHUNK), o == 1)
 
-        def gated(c):
-            cols = slice(c * CHUNK, (c + 1) * CHUNK)
-            for first, last in ((0, 2), (2, PACK)):
-                bank = pair_banks[2 * c + first // 2]
-                for r in range(first, last):
-                    for o in (1, 0):
-                        mx_pass(bank[:, r, :], LIN, o, r, cols, o == 1)
-                nc.vector.tensor_tensor(y[c][:, first:last, :], bank[:, first:last, :], gates[c // 2][:, first:last, (c % 2) * CHUNK : (c % 2 + 1) * CHUNK], MULT)
-            nc.sync.dma_start(out_rows[:, :, cols], y[c][:])
+        def gated_tile(r):
+            for c in range(2):
+                layer_sum(lin_banks[r][:, c, :], r, c)
+            nc.vector.tensor_tensor(y_low[:, r, :], lin_banks[r][:, 0:2, :].rearrange("p c q -> p (c q)"), gates[0][:, r, :], MULT)
+
+        def gated_chunk(c):
+            for pair in range(2):
+                bank = gate_banks[2 * (c - 2) + pair][:].rearrange("p (r q) -> p r q", r=PACK)
+                tiles = slice(2 * pair, 2 * pair + 2)
+                for r in range(tiles.start, tiles.stop):
+                    layer_sum(bank[:, r, :], r, c)
+                nc.vector.tensor_tensor(y[c][:, tiles, :], bank[:, tiles, :], gates[1][:, tiles, (c - 2) * CHUNK : (c - 1) * CHUNK], MULT)
+            nc.sync.dma_start(out_rows[:, :, c * CHUNK : (c + 1) * CHUNK], y[c])
 
         def round_result(engine_copy, c, first, last):
             engine_copy(*interleave_views(y_bf[:, c * CHUNK + first : c * CHUNK + last, :], y[c][:, :, first:last]))
@@ -178,13 +188,16 @@ def tile_attend_plh_bswiglu_topk_kernel(tc, qT, k_words, k_scales, c_words, c_sc
         def store_words(cols):
             nc.sync.dma_start(words_out[:, cols], y_codes[:, cols].bitcast(I32))
 
-        gated(0)
-        nc.gpsimd.tensor_scalar(y_bf[:, 0:CHUNK, :], y[0][:].rearrange("p t c -> p c t"), 1.0, 0.0, MULT, ADD)
-        for c in (1, 2):
-            gated(c)
-            round_result(nc.scalar.copy, c, 0, CHUNK)
+        for r in range(PACK):
+            gated_tile(r)
+            if r % 2:
+                nc.sync.dma_start(out_rows[:, r - 1 : r + 1, 0:HALF], y_low[:, r - 1 : r + 1, :])
+        nc.gpsimd.tensor_scalar(y_bf[:, 0:CHUNK, :], y[0].rearrange("p t c -> p c t"), 1.0, 0.0, MULT, ADD)
+        round_result(nc.scalar.copy, 1, 0, CHUNK)
+        gated_chunk(2)
+        round_result(nc.scalar.copy, 2, 0, CHUNK)
         quantise_result(slice(0, HALF))
-        gated(3)
+        gated_chunk(3)
         quantise_result(slice(HALF, HALF + CHUNK))
         store_words(slice(0, HALF + CHUNK))
         round_result(nc.scalar.copy, 3, 0, SCALAR_SHARE)

@@ -27,7 +27,6 @@ BANK = 512
 BIAS_ROW = P - 1
 SCALE_ROWS = (96, 32)
 GATE, LIN = 0, 1
-SCALAR_SHARE = 48
 
 
 def interleave_views(dst, src):
@@ -44,9 +43,7 @@ def tile_attend_plh_bswiglu_topk_kernel(tc, qT, k_words, k_scales, c_words, c_sc
         nb_pool = sb.tile([P, T], F32, name="nb_pool")
         k_pool = sb.tile([P, T], I32, name="k_pool", tag="after_k", align_bytes=64)
         scale_pools = [sb.tile([P, T], U8, name="scale_pool%d" % t) for t in range(2)]
-        q_first = sb.tile([P, PACK, NQ], F32, name="q_first")
-        q_early = sb.tile([P, PACK, HALF], F32, name="q_early")
-        q_late = sb.tile([P, PACK, HALF], F32, name="q_late")
+        q_raw = [sb.tile([P, PACK, NQ], F32, name="q_raw%d" % o) for o in range(PASSES)]
 
         warm_in = sb.tile([P, 1], F32, name="warm_in")
         warm_out = sb.tile([P, 1], F32, name="warm_out")
@@ -64,7 +61,7 @@ def tile_attend_plh_bswiglu_topk_kernel(tc, qT, k_words, k_scales, c_words, c_sc
         for pool, scales, row in zip(scale_pools, (k_scales, c_scales), SCALE_ROWS):
             nc.sync.dma_start(pool[row : row + 32, :].bitcast(I32), scales.rearrange("o f t -> f o t").bitcast(I32))
         nc.sync.dma_start(nb_pool[BIAS_ROW:P, :], nb[0:1, :])
-        nc.sync.dma_start(q_first[:], q_rows[0])
+        nc.sync.dma_start(q_raw[0][:], q_rows[0])
         nc.sync.dma_start(k_pool[:], k_words[0].rearrange("p t b -> p (t b)").bitcast(I32))
 
         planes = sb.tile([P, 2, PASSES, N], U8, name="planes", align_bytes=64)
@@ -85,8 +82,7 @@ def tile_attend_plh_bswiglu_topk_kernel(tc, qT, k_words, k_scales, c_words, c_sc
                 nc.sync.dma_start(planes[32 * quad : 32 * quad + 4, t].bitcast(I32), dealt[first : first + 8, t, :].bitcast(I32))
 
         place_scales(GATE)
-        nc.sync.dma_start(q_early[:], q_rows[1][:, :, 0:HALF])
-        nc.sync.dma_start(q_late[:], q_rows[1][:, :, HALF:NQ])
+        nc.sync.dma_start(q_raw[1][:], q_rows[1])
         c_pool = sb.tile([P, T], I32, name="c_pool")
         nc.sync.dma_start(c_pool[:], c_words[0].rearrange("p t b -> p (t b)").bitcast(I32))
         place_scales(LIN)
@@ -105,8 +101,8 @@ def tile_attend_plh_bswiglu_topk_kernel(tc, qT, k_words, k_scales, c_words, c_sc
         q_codes = [sb.tile([P, NQ], U32, name="q_codes%d" % o, tag=("" if o else "after_k"), align_bytes=64) for o in range(PASSES)]
         q_planes = [sb.tile([P, NQ], U8, name="q_plane%d" % o, align_bytes=64) for o in range(PASSES)]
 
-        def round_queries(engine_copy, o, cols, raw):
-            engine_copy(*interleave_views(q_bf[o][:, cols, :], raw[:]))
+        def round_queries(engine_copy, o, cols):
+            engine_copy(*interleave_views(q_bf[o][:, cols, :], q_raw[o][:, :, cols]))
 
         def quantise_queries(o, cols):
             nc.vector.quantize_mx(out=q_codes[o][:, cols].bitcast(FP8X4), scales=q_planes[o][:, cols], in_=q_bf[o][:, cols, :].rearrange("p w j -> p (w j)"))
@@ -120,13 +116,14 @@ def tile_attend_plh_bswiglu_topk_kernel(tc, qT, k_words, k_scales, c_words, c_sc
             nc.vector.tensor_copy(codes[:].bitcast(U16).rearrange("p o r s -> p o s r")[:, passes, :, tiles], halves[:, passes, :, tiles])
 
         w_codes = [sb.tile([P, PASSES, PACK, 2 * P], U8, name="w_codes%d" % t, tag=("after_gate" if t == GATE else ""), align_bytes=64) for t in range(2)]
-        round_queries(nc.scalar.copy, 0, slice(0, NQ), q_first)
+        round_queries(nc.scalar.copy, 0, slice(0, NQ))
         k_halves = gather_words("k", k_pool, "")
         deal_words(w_codes[GATE], k_halves, slice(0, 2), slice(0, 2))
         quantise_queries(0, slice(0, NQ))
         deal_words(w_codes[GATE], k_halves, slice(0, 2), slice(2, PACK))
-        round_queries(nc.scalar.copy, 1, slice(0, HALF), q_early)
-        round_queries(nc.vector.tensor_copy, 1, slice(HALF, NQ), q_late)
+        round_queries(nc.vector.tensor_copy, 1, slice(0, HALF))
+        round_queries(nc.vector.tensor_copy, 1, slice(HALF, HALF + 64))
+        round_queries(nc.scalar.copy, 1, slice(HALF + 64, NQ))
         quantise_queries(1, slice(0, HALF))
         quantise_queries(1, slice(HALF, NQ))
 
@@ -157,30 +154,29 @@ def tile_attend_plh_bswiglu_topk_kernel(tc, qT, k_words, k_scales, c_words, c_sc
         words_out = out_1[0].rearrange("p q b -> p (q b)").bitcast(I32)
         y_codes = sb.tile([P, NQ], U32, name="y_codes", align_bytes=64)
         y_plane = sb.tile([P, NQ], U8, name="y_plane", align_bytes=64)
-        y_low = sb.tile([P, PACK, HALF], F32, name="y_low")
-        y = [y_low[:, :, 0:CHUNK], y_low[:, :, CHUNK:HALF]] + [sb.tile([P, PACK, CHUNK], F32, name="y%d" % c)[:] for c in (2, 3)]
+        y = [sb.tile([P, PACK, HALF], F32, name="y%d" % h) for h in range(2)]
         y_bf = sb.tile([P, NQ, PACK], BF16, name="y_bf", align_bytes=64)
 
         def layer_sum(out, r, c):
             for o in (1, 0):
                 mx_pass(out, LIN, o, r, slice(c * CHUNK, (c + 1) * CHUNK), o == 1)
 
-        def gated_tile(r):
+        def gated_tile(bank, h, r):
             for c in range(2):
-                layer_sum(lin_banks[r][:, c, :], r, c)
-            nc.vector.tensor_tensor(y_low[:, r, :], lin_banks[r][:, 0:2, :].rearrange("p c q -> p (c q)"), gates[0][:, r, :], MULT)
+                layer_sum(bank[:, c, :], r, 2 * h + c)
+            nc.vector.tensor_tensor(y[h][:, r, :], bank[:, 0:2, :].rearrange("p c q -> p (c q)"), gates[h][:, r, :], MULT)
 
-        def gated_chunk(c):
-            for pair in range(2):
-                bank = gate_banks[2 * (c - 2) + pair][:].rearrange("p (r q) -> p r q", r=PACK)
-                tiles = slice(2 * pair, 2 * pair + 2)
-                for r in range(tiles.start, tiles.stop):
-                    layer_sum(bank[:, r, :], r, c)
-                nc.vector.tensor_tensor(y[c][:, tiles, :], bank[:, tiles, :], gates[1][:, tiles, (c - 2) * CHUNK : (c - 1) * CHUNK], MULT)
-            nc.sync.dma_start(out_rows[:, :, c * CHUNK : (c + 1) * CHUNK], y[c])
+        def gated_pair(bank, c):
+            cols = slice((c - 2) * CHUNK, (c - 1) * CHUNK)
+            for r in (2, 3):
+                layer_sum(bank[:, r, :], r, c)
+            nc.vector.tensor_tensor(y[1][:, 2:PACK, cols], bank[:, 2:PACK, :], gates[1][:, 2:PACK, cols], MULT)
 
-        def round_result(engine_copy, c, first, last):
-            engine_copy(*interleave_views(y_bf[:, c * CHUNK + first : c * CHUNK + last, :], y[c][:, :, first:last]))
+        def store_pair(h, first):
+            nc.sync.dma_start(out_rows[:, first : first + 2, h * HALF : (h + 1) * HALF], y[h][:, first : first + 2, :])
+
+        def round_result(engine_copy, h, cols, tiles):
+            engine_copy(*interleave_views(y_bf[:, h * HALF + cols.start : h * HALF + cols.stop, tiles], y[h][:, tiles, cols]))
 
         def quantise_result(cols):
             nc.vector.quantize_mx(out=y_codes[:, cols].bitcast(FP8X4), scales=y_plane[:, cols], in_=y_bf[:, cols, :].rearrange("p w j -> p (w j)"))
@@ -188,22 +184,29 @@ def tile_attend_plh_bswiglu_topk_kernel(tc, qT, k_words, k_scales, c_words, c_sc
         def store_words(cols):
             nc.sync.dma_start(words_out[:, cols], y_codes[:, cols].bitcast(I32))
 
+        spare = [bank[:].rearrange("p (r q) -> p r q", r=PACK) for bank in gate_banks]
+        left, right = slice(0, CHUNK), slice(CHUNK, HALF)
         for r in range(PACK):
-            gated_tile(r)
+            gated_tile(lin_banks[r], 0, r)
             if r % 2:
-                nc.sync.dma_start(out_rows[:, r - 1 : r + 1, 0:HALF], y_low[:, r - 1 : r + 1, :])
-        nc.gpsimd.tensor_scalar(y_bf[:, 0:CHUNK, :], y[0].rearrange("p t c -> p c t"), 1.0, 0.0, MULT, ADD)
-        round_result(nc.scalar.copy, 1, 0, CHUNK)
-        gated_chunk(2)
-        round_result(nc.scalar.copy, 2, 0, CHUNK)
+                store_pair(0, r - 1)
+        nc.gpsimd.tensor_scalar(y_bf[:, 0:CHUNK, :], y[0][:, :, left].rearrange("p t c -> p c t"), 1.0, 0.0, MULT, ADD)
+        round_result(nc.scalar.copy, 0, right, slice(0, PACK))
+        for r in range(2):
+            gated_tile(spare[r], 1, r)
+        store_pair(1, 0)
+        round_result(nc.scalar.copy, 1, left, slice(0, 2))
+        round_result(nc.scalar.copy, 1, right, slice(0, 2))
+        gated_pair(spare[2], 2)
+        gated_pair(spare[3], 3)
+        store_pair(1, 2)
+        round_result(nc.vector.tensor_copy, 1, left, slice(2, PACK))
         quantise_result(slice(0, HALF))
-        gated_chunk(3)
+        store_words(slice(0, HALF))
+        round_result(nc.vector.tensor_copy, 1, right, slice(2, PACK))
         quantise_result(slice(HALF, HALF + CHUNK))
-        store_words(slice(0, HALF + CHUNK))
-        round_result(nc.scalar.copy, 3, 0, SCALAR_SHARE)
-        round_result(nc.vector.tensor_copy, 3, SCALAR_SHARE, CHUNK)
         quantise_result(slice(HALF + CHUNK, NQ))
-        store_words(slice(HALF + CHUNK, NQ))
+        store_words(slice(HALF, NQ))
         for quad in range(4):
             queue = nc.scalar if quad % 2 else nc.sync
             queue.dma_start(out_2[0, 4 * quad : 4 * quad + 4, :].bitcast(I32), y_plane[32 * quad : 32 * quad + 4, :].bitcast(I32))

@@ -45,11 +45,6 @@ def tile_attend_plh_bswiglu_topk_kernel(tc, qT, k_words, k_scales, c_words, c_sc
         scale_pools = [sb.tile([P, T], U8, name="scale_pool%d" % t) for t in range(2)]
         q_raw = [sb.tile([P, PACK, NQ], F32, name="q_raw%d" % o) for o in range(PASSES)]
 
-        warm_in = sb.tile([P, 1], F32, name="warm_in")
-        warm_out = sb.tile([P, 1], F32, name="warm_out")
-        nc.gpsimd.memset(warm_in[:], 0.0)
-        nc.scalar.activation(warm_out[:], warm_in[:], SILU)
-
         nc.gpsimd.memset(scale_pools[GATE][0:96, :].bitcast(I32), 0)
         nc.gpsimd.memset(scale_pools[LIN][0:32, :].bitcast(I32), 0)
         nc.gpsimd.memset(scale_pools[LIN][64:P, :].bitcast(I32), 0)

@@ -23,7 +23,6 @@ PACK = 4
 PASSES = 2
 HALF = NQ // 2
 CHUNK = 128
-BANK = 512
 BIAS_ROW = P - 1
 SCALE_ROWS = (96, 32)
 GATE, LIN = 0, 1
@@ -41,9 +40,13 @@ def tile_attend_plh_bswiglu_topk_kernel(tc, qT, k_words, k_scales, c_words, c_sc
 
         offsets = sb.tile([P, N // 16], U16, name="offsets")
         nb_pool = sb.tile([P, T], F32, name="nb_pool")
-        k_pool = sb.tile([P, T], I32, name="k_pool", tag="after_k", align_bytes=64)
-        scale_pools = [sb.tile([P, T], U8, name="scale_pool%d" % t) for t in range(2)]
-        q_raw = [sb.tile([P, PACK, NQ], F32, name="q_raw%d" % o) for o in range(PASSES)]
+        k_pool = sb.tile([P, T], I32, name="k_pool", align_bytes=64)
+        scale_pools = [sb.tile([P, T], U8, name="scale_pool%d" % t, align_bytes=64) for t in range(2)]
+        pieces = [(0, slice(0, HALF)), (0, slice(HALF, NQ)), (1, slice(0, HALF)), (1, slice(HALF, NQ))]
+        q_first = sb.tile([P, PACK, NQ], F32, name="q_first")
+        q_early = sb.tile([P, PACK, HALF], F32, name="q_early")
+        q_late = sb.tile([P, PACK, HALF], F32, name="q_late", tag="late")
+        q_raw = [q_first[:, :, 0:HALF], q_first[:, :, HALF:NQ], q_early[:], q_late[:]]
 
         nc.gpsimd.memset(scale_pools[GATE][0:96, :].bitcast(I32), 0)
         nc.gpsimd.memset(scale_pools[LIN][0:32, :].bitcast(I32), 0)
@@ -56,7 +59,7 @@ def tile_attend_plh_bswiglu_topk_kernel(tc, qT, k_words, k_scales, c_words, c_sc
         for pool, scales, row in zip(scale_pools, (k_scales, c_scales), SCALE_ROWS):
             nc.sync.dma_start(pool[row : row + 32, :].bitcast(I32), scales.rearrange("o f t -> f o t").bitcast(I32))
         nc.sync.dma_start(nb_pool[BIAS_ROW:P, :], nb[0:1, :])
-        nc.sync.dma_start(q_raw[0][:], q_rows[0])
+        nc.sync.dma_start(q_first[:], q_rows[0])
         nc.sync.dma_start(k_pool[:], k_words[0].rearrange("p t b -> p (t b)").bitcast(I32))
 
         planes = sb.tile([P, 2, PASSES, N], U8, name="planes", align_bytes=64)
@@ -65,26 +68,33 @@ def tile_attend_plh_bswiglu_topk_kernel(tc, qT, k_words, k_scales, c_words, c_sc
         make_identity(nc, ident[:])
 
         picked_scales = [sb.tile([P, N], U8, name="picked_scales%d" % t) for t in range(2)]
-        dealt = sb.tile([P, 2, N], U8, name="dealt")
-        for t in range(2):
+        dealt = [sb.tile([P, N], U8, name="dealt%d" % t) for t in range(2)]
+
+        def gather_scales(t):
             nc.vector.tensor_copy(picked_scales[t][:], scale_pools[t][:].indirect(offsets[:]))
+
+        def deal_scales(t):
+            nc.vector.tensor_copy(dealt[t][:].rearrange("p (r s) -> p r s", r=PACK), picked_scales[t][:].rearrange("p (s r) -> p r s", r=PACK))
+
         for t in range(2):
-            nc.vector.tensor_copy(dealt[:, t, :].rearrange("p (r s) -> p r s", r=PACK), picked_scales[t][:].rearrange("p (s r) -> p r s", r=PACK))
+            gather_scales(t)
+            deal_scales(t)
 
         def place_scales(t):
             for quad in (0, 2, 1, 3):
                 first = SCALE_ROWS[t] + 8 * quad
-                nc.sync.dma_start(planes[32 * quad : 32 * quad + 4, t].bitcast(I32), dealt[first : first + 8, t, :].bitcast(I32))
+                nc.sync.dma_start(planes[32 * quad : 32 * quad + 4, t].bitcast(I32), dealt[t][first : first + 8, :].bitcast(I32))
 
         place_scales(GATE)
-        nc.sync.dma_start(q_raw[1][:], q_rows[1])
+        nc.sync.dma_start(q_early[:], q_rows[1][:, :, 0:HALF])
         c_pool = sb.tile([P, T], I32, name="c_pool")
         nc.sync.dma_start(c_pool[:], c_words[0].rearrange("p t b -> p (t b)").bitcast(I32))
         place_scales(LIN)
+        nc.sync.dma_start(q_late[:], q_rows[1][:, :, HALF:NQ])
         nb_picked = sb.tile([P, N], F32, name="nb_picked")
         nc.vector.tensor_copy(nb_picked[:], nb_pool[:].indirect(offsets[:]))
 
-        gate_banks = [psum.tile([P, NQ], F32, name="gate%d" % r) for r in range(PACK)]
+        gate_banks = [psum.tile([P, PACK, CHUNK], F32, name="gate%d" % b) for b in range(4)]
         lin_banks = [psum.tile([P, PACK, CHUNK], F32, name="lin%d" % c) for c in range(4)]
         nb_turned = lin_banks[3]
         for r in range(PACK):
@@ -92,15 +102,16 @@ def tile_attend_plh_bswiglu_topk_kernel(tc, qT, k_words, k_scales, c_words, c_sc
         bias = sb.tile([P, PACK], F32, name="bias")
         nc.scalar.copy(bias[:], nb_turned[:, :, BIAS_ROW])
 
-        q_bf = [sb.tile([P, NQ, PACK], BF16, name="q_bf%d" % o, align_bytes=64) for o in range(PASSES)]
-        q_codes = [sb.tile([P, NQ], U32, name="q_codes%d" % o, tag=("" if o else "after_k"), align_bytes=64) for o in range(PASSES)]
+        q_bf = [sb.tile([P, cols.stop - cols.start, PACK], BF16, name="q_bf%d" % i, align_bytes=64) for i, (o, cols) in enumerate(pieces)]
+        q_codes = [sb.tile([P, NQ], U32, name="q_codes%d" % o, align_bytes=64) for o in range(PASSES)]
         q_planes = [sb.tile([P, NQ], U8, name="q_plane%d" % o, align_bytes=64) for o in range(PASSES)]
 
-        def round_queries(engine_copy, o, cols):
-            engine_copy(*interleave_views(q_bf[o][:, cols, :], q_raw[o][:, :, cols]))
+        def round_queries(engine_copy, i):
+            engine_copy(*interleave_views(q_bf[i][:], q_raw[i]))
 
-        def quantise_queries(o, cols):
-            nc.vector.quantize_mx(out=q_codes[o][:, cols].bitcast(FP8X4), scales=q_planes[o][:, cols], in_=q_bf[o][:, cols, :].rearrange("p w j -> p (w j)"))
+        def quantise_queries(i):
+            o, cols = pieces[i]
+            nc.vector.quantize_mx(out=q_codes[o][:, cols].bitcast(FP8X4), scales=q_planes[o][:, cols], in_=q_bf[i][:].rearrange("p w j -> p (w j)"))
 
         def gather_words(name, pool, tag):
             picked = sb.tile([P, N], U32, name=name + "_picked", tag=tag)
@@ -110,95 +121,102 @@ def tile_attend_plh_bswiglu_topk_kernel(tc, qT, k_words, k_scales, c_words, c_sc
         def deal_words(codes, halves, passes, tiles):
             nc.vector.tensor_copy(codes[:].bitcast(U16).rearrange("p o r s -> p o s r")[:, passes, :, tiles], halves[:, passes, :, tiles])
 
-        w_codes = [sb.tile([P, PASSES, PACK, 2 * P], U8, name="w_codes%d" % t, tag=("after_gate" if t == GATE else ""), align_bytes=64) for t in range(2)]
-        round_queries(nc.scalar.copy, 0, slice(0, NQ))
+        w_codes = [sb.tile([P, PASSES, PACK, 2 * P], U8, name="w_codes%d" % t, align_bytes=64) for t in range(2)]
+        round_queries(nc.scalar.copy, 0)
+        round_queries(nc.scalar.copy, 1)
+        quantise_queries(0)
+        for r in range(3):
+            nc.tensor.matmul_mx(
+                out=gate_banks[r][:].rearrange("p r q -> p (r q)"),
+                lhsT=q_codes[0][:, 0:P].bitcast(FP8X4),
+                lhsT_scale=q_planes[0][:, 0:P],
+                rhs=k_pool[:].bitcast(U8)[:, 0 : 2 * NQ].bitcast(FP4X4),
+                rhs_scale=scale_pools[GATE][:, 0:NQ],
+                start=True,
+                stop=True,
+            )
         k_halves = gather_words("k", k_pool, "")
+        quantise_queries(1)
         deal_words(w_codes[GATE], k_halves, slice(0, 2), slice(0, 2))
-        quantise_queries(0, slice(0, NQ))
         deal_words(w_codes[GATE], k_halves, slice(0, 2), slice(2, PACK))
-        round_queries(nc.vector.tensor_copy, 1, slice(0, HALF))
-        round_queries(nc.vector.tensor_copy, 1, slice(HALF, HALF + 64))
-        round_queries(nc.scalar.copy, 1, slice(HALF + 64, NQ))
-        quantise_queries(1, slice(0, HALF))
-        quantise_queries(1, slice(HALF, NQ))
+        round_queries(nc.scalar.copy, 2)
+        quantise_queries(2)
 
-        def mx_pass(out, t, o, r, cols, first):
+        def mx_pass(out, t, o, r, cols, start, stop):
             nc.tensor.matmul_mx(
                 out=out,
                 lhsT=w_codes[t][:, o, r, :].bitcast(FP4X4),
                 lhsT_scale=planes[:, t, o, P * r : P * (r + 1)],
                 rhs=q_codes[o][:, cols].bitcast(FP8X4),
                 rhs_scale=q_planes[o][:, cols],
-                start=first,
-                stop=not first,
+                start=start,
+                stop=stop,
             )
 
-        for o in range(PASSES):
+        gates = [[sb.tile([P, 2, HALF], F32, name="gates%d%d" % (h, pair), tag=("last_gates" if (h, pair) == (1, 0) else ""), align_bytes=64) for pair in range(2)] for h in range(2)]
+
+        def gate_passes(h, o):
+            for pair in range(2):
+                for i in range(4):
+                    r, c = 2 * pair + i // 2, 2 * h + i % 2
+                    mx_pass(gate_banks[2 * h + pair][:, i, :], GATE, o, r, slice(c * CHUNK, (c + 1) * CHUNK), o == 0 and i == 0, o == 1 and i == 3)
+
+        def activate(h):
             for r in range(PACK):
-                mx_pass(gate_banks[r][:], GATE, o, r, slice(0, NQ), o == 0)
-        gates = [sb.tile([P, PACK, HALF], F32, name="gates%d" % h, tag=("after_gate" if h else ""), align_bytes=64) for h in range(2)]
-        for h in range(2):
-            for r in range(PACK):
-                nc.scalar.activation(gates[h][:, r, :], gate_banks[r][:, h * HALF : (h + 1) * HALF], SILU, bias=bias[:, r : r + 1])
+                sums = gate_banks[2 * h + r // 2][:, 2 * (r % 2) : 2 * (r % 2) + 2, :].rearrange("p c q -> p (c q)")
+                nc.scalar.activation(gates[h][r // 2][:, r % 2, :], sums, SILU, bias=bias[:, r : r + 1])
+
+        gate_passes(0, 0)
+        gate_passes(0, 1)
+        activate(0)
+        gate_passes(1, 0)
 
         c_halves = gather_words("c", c_pool, "")
         deal_words(w_codes[LIN], c_halves, slice(0, 2), slice(0, 2))
         deal_words(w_codes[LIN], c_halves, slice(0, 2), slice(2, PACK))
+        round_queries(nc.vector.tensor_copy, 3)
+        quantise_queries(3)
 
         out_rows = out_0.rearrange("(p r) q -> p r q", r=PACK)
         words_out = out_1[0].rearrange("p q b -> p (q b)").bitcast(I32)
-        y_codes = sb.tile([P, NQ], U32, name="y_codes", align_bytes=64)
         y_plane = sb.tile([P, NQ], U8, name="y_plane", align_bytes=64)
-        y = [sb.tile([P, PACK, HALF], F32, name="y%d" % h) for h in range(2)]
+        y_halves = [sb.tile([P, PACK, HALF], F32, name="y%d" % h, tag=("" if h else "late")) for h in range(2)]
+        y = [y_halves[c // 2][:, :, (c % 2) * CHUNK : (c % 2 + 1) * CHUNK] for c in range(4)]
         y_bf = sb.tile([P, NQ, PACK], BF16, name="y_bf", align_bytes=64)
 
-        def layer_sum(out, r, c):
-            for o in (1, 0):
-                mx_pass(out, LIN, o, r, slice(c * CHUNK, (c + 1) * CHUNK), o == 1)
+        def gated_pair(c, first):
+            bank = lin_banks[(2 * c + first // 2) % 4]
+            cols = slice(c * CHUNK, (c + 1) * CHUNK)
+            for r in range(first, first + 2):
+                for o in (1, 0):
+                    mx_pass(bank[:, r, :], LIN, o, r, cols, o == 1, o == 0)
+            nc.vector.tensor_tensor(y[c][:, first : first + 2, :], bank[:, first : first + 2, :], gates[c // 2][first // 2][:, :, (c % 2) * CHUNK : (c % 2 + 1) * CHUNK], MULT)
 
-        def gated_tile(bank, h, r):
-            for c in range(2):
-                layer_sum(bank[:, c, :], r, 2 * h + c)
-            nc.vector.tensor_tensor(y[h][:, r, :], bank[:, 0:2, :].rearrange("p c q -> p (c q)"), gates[h][:, r, :], MULT)
-
-        def gated_pair(bank, c):
-            cols = slice((c - 2) * CHUNK, (c - 1) * CHUNK)
-            for r in (2, 3):
-                layer_sum(bank[:, r, :], r, c)
-            nc.vector.tensor_tensor(y[1][:, 2:PACK, cols], bank[:, 2:PACK, :], gates[1][:, 2:PACK, cols], MULT)
-
-        def store_pair(h, first):
-            nc.sync.dma_start(out_rows[:, first : first + 2, h * HALF : (h + 1) * HALF], y[h][:, first : first + 2, :])
-
-        def round_result(engine_copy, h, cols, tiles):
-            engine_copy(*interleave_views(y_bf[:, h * HALF + cols.start : h * HALF + cols.stop, tiles], y[h][:, tiles, cols]))
+        def round_result(engine_copy, c, cols):
+            engine_copy(*interleave_views(y_bf[:, c * CHUNK + cols.start : c * CHUNK + cols.stop, :], y[c][:, :, cols]))
 
         def quantise_result(cols):
-            nc.vector.quantize_mx(out=y_codes[:, cols].bitcast(FP8X4), scales=y_plane[:, cols], in_=y_bf[:, cols, :].rearrange("p w j -> p (w j)"))
+            nc.vector.quantize_mx(out=y_codes[cols.start // HALF][:, cols.start % HALF : (cols.stop - 1) % HALF + 1].bitcast(FP8X4), scales=y_plane[:, cols], in_=y_bf[:, cols, :].rearrange("p w j -> p (w j)"))
 
         def store_words(cols):
-            nc.sync.dma_start(words_out[:, cols], y_codes[:, cols].bitcast(I32))
+            nc.sync.dma_start(words_out[:, cols], y_codes[cols.start // HALF][:].bitcast(I32))
 
-        spare = [bank[:].rearrange("p (r q) -> p r q", r=PACK) for bank in gate_banks]
-        left, right = slice(0, CHUNK), slice(CHUNK, HALF)
-        for r in range(PACK):
-            gated_tile(lin_banks[r], 0, r)
-            if r % 2:
-                store_pair(0, r - 1)
-        nc.gpsimd.tensor_scalar(y_bf[:, 0:CHUNK, :], y[0][:, :, left].rearrange("p t c -> p c t"), 1.0, 0.0, MULT, ADD)
-        round_result(nc.scalar.copy, 0, right, slice(0, PACK))
-        for r in range(2):
-            gated_tile(spare[r], 1, r)
-        store_pair(1, 0)
-        round_result(nc.scalar.copy, 1, left, slice(0, 2))
-        round_result(nc.scalar.copy, 1, right, slice(0, 2))
-        gated_pair(spare[2], 2)
-        gated_pair(spare[3], 3)
-        store_pair(1, 2)
-        round_result(nc.vector.tensor_copy, 1, left, slice(2, PACK))
+        for c in range(4):
+            if c == 2:
+                gate_passes(1, 1)
+                activate(1)
+            gated_pair(c, 0)
+            gated_pair(c, 2)
+            nc.sync.dma_start(out_rows[:, :, c * CHUNK : (c + 1) * CHUNK], y[c])
+            if c < 2:
+                nc.gpsimd.tensor_scalar(y_bf[:, c * CHUNK : (c + 1) * CHUNK, :], y[c].rearrange("p t c -> p c t"), 1.0, 0.0, MULT, ADD)
+            elif c < 3:
+                round_result(nc.scalar.copy, c, slice(0, CHUNK))
+        y_codes = [sb.tile([P, HALF], U32, name="y_codes%d" % h, tag=("" if h else "last_gates"), align_bytes=64) for h in range(2)]
+        round_result(nc.scalar.copy, 3, slice(0, 48))
         quantise_result(slice(0, HALF))
         store_words(slice(0, HALF))
-        round_result(nc.vector.tensor_copy, 1, right, slice(2, PACK))
+        round_result(nc.vector.tensor_copy, 3, slice(48, CHUNK))
         quantise_result(slice(HALF, HALF + CHUNK))
         quantise_result(slice(HALF + CHUNK, NQ))
         store_words(slice(HALF, NQ))

@@ -153,7 +153,7 @@ def tile_attend_plh_bswiglu_topk_kernel(tc, qT, k_words, k_scales, c_words, c_sc
                 stop=stop,
             )
 
-        gates = [[sb.tile([P, 2, HALF], F32, name="gates%d%d" % (h, pair), tag=("last_gates" if (h, pair) == (1, 0) else ""), align_bytes=64) for pair in range(2)] for h in range(2)]
+        gates = [[sb.tile([P, 2, HALF], F32, name="gates%d%d" % (h, pair), tag=("last_gates" if (h, pair) == (1, 1) else ""), align_bytes=64) for pair in range(2)] for h in range(2)]
 
         def gate_passes(h, o):
             for pair in range(2):
@@ -180,46 +180,50 @@ def tile_attend_plh_bswiglu_topk_kernel(tc, qT, k_words, k_scales, c_words, c_sc
         out_rows = out_0.rearrange("(p r) q -> p r q", r=PACK)
         words_out = out_1[0].rearrange("p q b -> p (q b)").bitcast(I32)
         y_plane = sb.tile([P, NQ], U8, name="y_plane", align_bytes=64)
-        y_halves = [sb.tile([P, PACK, HALF], F32, name="y%d" % h, tag=("" if h else "late")) for h in range(2)]
-        y = [y_halves[c // 2][:, :, (c % 2) * CHUNK : (c % 2 + 1) * CHUNK] for c in range(4)]
+        y = [sb.tile([P, PACK, HALF], F32, name="y%d" % h, tag=("" if h else "late")) for h in range(2)]
         y_bf = sb.tile([P, NQ, PACK], BF16, name="y_bf", align_bytes=64)
 
-        def gated_pair(c, first):
-            bank = lin_banks[(2 * c + first // 2) % 4]
-            cols = slice(c * CHUNK, (c + 1) * CHUNK)
-            for r in range(first, first + 2):
-                for o in (1, 0):
-                    mx_pass(bank[:, r, :], LIN, o, r, cols, o == 1, o == 0)
-            nc.vector.tensor_tensor(y[c][:, first : first + 2, :], bank[:, first : first + 2, :], gates[c // 2][first // 2][:, :, (c % 2) * CHUNK : (c % 2 + 1) * CHUNK], MULT)
+        def layer_sum(out, r, c):
+            for o in (1, 0):
+                mx_pass(out, LIN, o, r, slice(c * CHUNK, (c + 1) * CHUNK), o == 1, o == 0)
 
-        def round_result(engine_copy, c, cols):
-            engine_copy(*interleave_views(y_bf[:, c * CHUNK + cols.start : c * CHUNK + cols.stop, :], y[c][:, :, cols]))
+        def gated_tile(bank, h, r):
+            for c in range(2):
+                layer_sum(bank[:, c, :], r, 2 * h + c)
+            nc.vector.tensor_tensor(y[h][:, r, :], bank[:, 0:2, :].rearrange("p c q -> p (c q)"), gates[h][r // 2][:, r % 2, :], MULT)
+            nc.sync.dma_start(out_rows[:, r, h * HALF : (h + 1) * HALF], y[h][:, r, :])
 
-        def quantise_result(cols):
-            nc.vector.quantize_mx(out=y_codes[cols.start // HALF][:, cols.start % HALF : (cols.stop - 1) % HALF + 1].bitcast(FP8X4), scales=y_plane[:, cols], in_=y_bf[:, cols, :].rearrange("p w j -> p (w j)"))
+        def gated_pair(bank, cols, c):
+            for r in (2, 3):
+                layer_sum(bank[:, r, :], r, c)
+            nc.vector.tensor_tensor(y[1][:, 2:PACK, cols], bank[:, 2:PACK, :], gates[1][1][:, :, cols], MULT)
 
-        def store_words(cols):
-            nc.sync.dma_start(words_out[:, cols], y_codes[cols.start // HALF][:].bitcast(I32))
+        def round_result(engine_copy, h, cols, tiles):
+            engine_copy(*interleave_views(y_bf[:, h * HALF + cols.start : h * HALF + cols.stop, tiles], y[h][:, tiles, cols]))
 
-        for c in range(4):
-            if c == 2:
-                gate_passes(1, 1)
-                activate(1)
-            gated_pair(c, 0)
-            gated_pair(c, 2)
-            nc.sync.dma_start(out_rows[:, :, c * CHUNK : (c + 1) * CHUNK], y[c])
-            if c < 2:
-                nc.gpsimd.tensor_scalar(y_bf[:, c * CHUNK : (c + 1) * CHUNK, :], y[c].rearrange("p t c -> p c t"), 1.0, 0.0, MULT, ADD)
-            elif c < 3:
-                round_result(nc.scalar.copy, c, slice(0, CHUNK))
+        def quantise_result(h):
+            cols = slice(h * HALF, (h + 1) * HALF)
+            nc.vector.quantize_mx(out=y_codes[h][:].bitcast(FP8X4), scales=y_plane[:, cols], in_=y_bf[:, cols, :].rearrange("p w j -> p (w j)"))
+            nc.sync.dma_start(words_out[:, cols], y_codes[h][:].bitcast(I32))
+
+        left, right = slice(0, CHUNK), slice(CHUNK, HALF)
+        for r in range(PACK):
+            gated_tile(lin_banks[r], 0, r)
+        for cols in (left, right):
+            nc.gpsimd.tensor_scalar(y_bf[:, cols, :], y[0][:, :, cols].rearrange("p t c -> p c t"), 1.0, 0.0, MULT, ADD)
+        gate_passes(1, 1)
+        activate(1)
+        for r in range(2):
+            gated_tile(lin_banks[r], 1, r)
+        round_result(nc.scalar.copy, 1, slice(0, HALF), slice(0, 2))
+        gated_pair(lin_banks[2], left, 2)
+        gated_pair(lin_banks[3], right, 3)
+        nc.sync.dma_start(out_rows[:, 2:PACK, HALF:NQ], y[1][:, 2:PACK, :])
         y_codes = [sb.tile([P, HALF], U32, name="y_codes%d" % h, tag=("" if h else "last_gates"), align_bytes=64) for h in range(2)]
-        round_result(nc.scalar.copy, 3, slice(0, 48))
-        quantise_result(slice(0, HALF))
-        store_words(slice(0, HALF))
-        round_result(nc.vector.tensor_copy, 3, slice(48, CHUNK))
-        quantise_result(slice(HALF, HALF + CHUNK))
-        quantise_result(slice(HALF + CHUNK, NQ))
-        store_words(slice(HALF, NQ))
+        round_result(nc.vector.tensor_copy, 1, left, slice(2, PACK))
+        round_result(nc.vector.tensor_copy, 1, right, slice(2, PACK))
+        quantise_result(0)
+        quantise_result(1)
         for quad in range(4):
             queue = nc.scalar if quad % 2 else nc.sync
             queue.dma_start(out_2[0, 4 * quad : 4 * quad + 4, :].bitcast(I32), y_plane[32 * quad : 32 * quad + 4, :].bitcast(I32))

@@ -125,16 +125,6 @@ def tile_attend_plh_bswiglu_topk_kernel(tc, qT, k_words, k_scales, c_words, c_sc
         round_queries(nc.scalar.copy, 0)
         round_queries(nc.scalar.copy, 1)
         quantise_queries(0)
-        for r in range(3):
-            nc.tensor.matmul_mx(
-                out=gate_banks[r][:].rearrange("p r q -> p (r q)"),
-                lhsT=q_codes[0][:, 0:P].bitcast(FP8X4),
-                lhsT_scale=q_planes[0][:, 0:P],
-                rhs=k_pool[:].bitcast(U8)[:, 0 : 2 * NQ].bitcast(FP4X4),
-                rhs_scale=scale_pools[GATE][:, 0:NQ],
-                start=True,
-                stop=True,
-            )
         k_halves = gather_words("k", k_pool, "")
         quantise_queries(1)
         deal_words(w_codes[GATE], k_halves, slice(0, 2), slice(0, 2))
@@ -191,7 +181,9 @@ def tile_attend_plh_bswiglu_topk_kernel(tc, qT, k_words, k_scales, c_words, c_sc
             for c in range(2):
                 layer_sum(bank[:, c, :], r, 2 * h + c)
             nc.vector.tensor_tensor(y[h][:, r, :], bank[:, 0:2, :].rearrange("p c q -> p (c q)"), gates[h][r // 2][:, r % 2, :], MULT)
-            nc.sync.dma_start(out_rows[:, r, h * HALF : (h + 1) * HALF], y[h][:, r, :])
+
+        def store_tiles(h, tiles):
+            nc.sync.dma_start(out_rows[:, tiles, h * HALF : (h + 1) * HALF], y[h][:, tiles, :])
 
         def gated_pair(bank, cols, c):
             for r in (2, 3):
@@ -209,16 +201,19 @@ def tile_attend_plh_bswiglu_topk_kernel(tc, qT, k_words, k_scales, c_words, c_sc
         left, right = slice(0, CHUNK), slice(CHUNK, HALF)
         for r in range(PACK):
             gated_tile(lin_banks[r], 0, r)
-        for cols in (left, right):
-            nc.gpsimd.tensor_scalar(y_bf[:, cols, :], y[0][:, :, cols].rearrange("p t c -> p c t"), 1.0, 0.0, MULT, ADD)
+            if r % 2:
+                store_tiles(0, slice(r - 1, r + 1))
+        nc.gpsimd.tensor_scalar(y_bf[:, 0:192, :], y[0][:, :, 0:192].rearrange("p t c -> p c t"), 1.0, 0.0, MULT, ADD)
         gate_passes(1, 1)
         activate(1)
+        round_result(nc.scalar.copy, 0, slice(192, HALF), slice(0, PACK))
         for r in range(2):
             gated_tile(lin_banks[r], 1, r)
+        store_tiles(1, slice(0, 2))
         round_result(nc.scalar.copy, 1, slice(0, HALF), slice(0, 2))
         gated_pair(lin_banks[2], left, 2)
         gated_pair(lin_banks[3], right, 3)
-        nc.sync.dma_start(out_rows[:, 2:PACK, HALF:NQ], y[1][:, 2:PACK, :])
+        store_tiles(1, slice(2, PACK))
         y_codes = [sb.tile([P, HALF], U32, name="y_codes%d" % h, tag=("" if h else "last_gates"), align_bytes=64) for h in range(2)]
         round_result(nc.vector.tensor_copy, 1, left, slice(2, PACK))
         round_result(nc.vector.tensor_copy, 1, right, slice(2, PACK))

@@ -15,6 +15,7 @@ U8 = mybir.dt.uint8
 FP8X4 = mybir.dt.float8_e4m3fn_x4
 FP4X4 = mybir.dt.float4_e2m1fn_x4
 SILU = mybir.ActivationFunctionType.Silu
+COPY = mybir.ActivationFunctionType.Copy
 MULT = mybir.AluOpType.mult
 ADD = mybir.AluOpType.add
 
@@ -40,45 +41,42 @@ def tile_attend_plh_bswiglu_topk_kernel(tc, qT, k_words, k_scales, c_words, c_sc
 
         offsets = sb.tile([P, N // 16], U16, name="offsets")
         nb_pool = sb.tile([P, T], F32, name="nb_pool")
-        k_pool = sb.tile([P, T], I32, name="k_pool", align_bytes=64)
+        word_pools = [sb.tile([P, T], I32, name="word_pool%d" % t, align_bytes=64) for t in range(2)]
         scale_pools = [sb.tile([P, T], U8, name="scale_pool%d" % t, align_bytes=64) for t in range(2)]
-        pieces = [(0, slice(0, HALF)), (0, slice(HALF, NQ)), (1, slice(0, HALF)), (1, slice(HALF, NQ))]
-        q_first = sb.tile([P, PACK, NQ], F32, name="q_first")
-        q_early = sb.tile([P, PACK, HALF], F32, name="q_early")
-        q_late = sb.tile([P, PACK, HALF], F32, name="q_late", tag="late")
-        q_raw = [q_first[:, :, 0:HALF], q_first[:, :, HALF:NQ], q_early[:], q_late[:]]
+        q_raw = [[sb.tile([P, PACK, HALF], F32, name="q_raw%d%d" % (h, o), tag="q_raw%d%d" % (h, o), align_bytes=64) for o in range(PASSES)] for h in range(2)]
+        planes = sb.tile([P, 2, PASSES, N], U8, name="planes", align_bytes=64)
+        ident = sb.tile([P, P], F32, name="ident")
 
+        warm = sb.tile([P, 2], F32, name="warm")
+        nc.gpsimd.memset(warm[:, 0:1], 0.0)
+        nc.scalar.activation(warm[:, 1:2], warm[:, 0:1], SILU)
         nc.gpsimd.memset(scale_pools[GATE][0:96, :].bitcast(I32), 0)
         nc.gpsimd.memset(scale_pools[LIN][0:32, :].bitcast(I32), 0)
         nc.gpsimd.memset(scale_pools[LIN][64:P, :].bitcast(I32), 0)
         for cols in (slice(0, T - 1), slice(T - 1, T)):
             nc.vector.memset(nb_pool[0:BIAS_ROW, cols].bitcast(I32), 0)
+        make_identity(nc, ident[:])
+        nc.gpsimd.memset(planes[:].bitcast(I32), 0)
 
         q_rows = qT[0].rearrange("(o p j) w -> o p j w", o=PASSES, j=PACK)
+
+        def load_queries(h, o):
+            nc.sync.dma_start(q_raw[h][o][:], q_rows[o][:, :, h * HALF : (h + 1) * HALF])
+
+        def load_words(t, words):
+            nc.sync.dma_start(word_pools[t][:], words[0].rearrange("p t b -> p (t b)").bitcast(I32))
+
         nc.sync.dma_start(offsets[:], offs)
-        for pool, scales, row in zip(scale_pools, (k_scales, c_scales), SCALE_ROWS):
-            nc.sync.dma_start(pool[row : row + 32, :].bitcast(I32), scales.rearrange("o f t -> f o t").bitcast(I32))
+        for queue, pool, scales, row in zip((nc.sync, nc.sync), scale_pools, (k_scales, c_scales), SCALE_ROWS):
+            queue.dma_start(pool[row : row + 32, :].bitcast(I32), scales.rearrange("o f t -> f o t").bitcast(I32))
         nc.sync.dma_start(nb_pool[BIAS_ROW:P, :], nb[0:1, :])
-        nc.sync.dma_start(q_first[:], q_rows[0])
-        nc.sync.dma_start(k_pool[:], k_words[0].rearrange("p t b -> p (t b)").bitcast(I32))
+        load_words(GATE, k_words)
+        load_queries(0, 0)
+        load_queries(0, 1)
 
-        planes = sb.tile([P, 2, PASSES, N], U8, name="planes", align_bytes=64)
-        nc.gpsimd.memset(planes[:].bitcast(I32), 0)
-        ident = sb.tile([P, P], F32, name="ident")
-        make_identity(nc, ident[:])
-
-        picked_scales = [sb.tile([P, N], U8, name="picked_scales%d" % t) for t in range(2)]
         dealt = [sb.tile([P, N], U8, name="dealt%d" % t) for t in range(2)]
-
-        def gather_scales(t):
-            nc.vector.tensor_copy(picked_scales[t][:], scale_pools[t][:].indirect(offsets[:]))
-
-        def deal_scales(t):
-            nc.vector.tensor_copy(dealt[t][:].rearrange("p (r s) -> p r s", r=PACK), picked_scales[t][:].rearrange("p (s r) -> p r s", r=PACK))
-
         for t in range(2):
-            gather_scales(t)
-            deal_scales(t)
+            nc.vector.tensor_copy(dealt[t][:].rearrange("p (r s) -> p s r", r=PACK), scale_pools[t][:].indirect(offsets[:]))
 
         def place_scales(t):
             for quad in (0, 2, 1, 3):
@@ -86,139 +84,145 @@ def tile_attend_plh_bswiglu_topk_kernel(tc, qT, k_words, k_scales, c_words, c_sc
                 nc.sync.dma_start(planes[32 * quad : 32 * quad + 4, t].bitcast(I32), dealt[t][first : first + 8, :].bitcast(I32))
 
         place_scales(GATE)
-        nc.sync.dma_start(q_early[:], q_rows[1][:, :, 0:HALF])
-        c_pool = sb.tile([P, T], I32, name="c_pool")
-        nc.sync.dma_start(c_pool[:], c_words[0].rearrange("p t b -> p (t b)").bitcast(I32))
+        load_words(LIN, c_words)
         place_scales(LIN)
-        nc.sync.dma_start(q_late[:], q_rows[1][:, :, HALF:NQ])
-        nb_picked = sb.tile([P, N], F32, name="nb_picked")
-        nc.vector.tensor_copy(nb_picked[:], nb_pool[:].indirect(offsets[:]))
+        load_queries(1, 0)
+        load_queries(1, 1)
 
-        gate_banks = [psum.tile([P, PACK, CHUNK], F32, name="gate%d" % b) for b in range(4)]
-        lin_banks = [psum.tile([P, PACK, CHUNK], F32, name="lin%d" % c) for c in range(4)]
-        nb_turned = lin_banks[3]
+        banks = [psum.tile([P, 2, HALF], F32, name="bank%d" % b) for b in range(8)]
+        gate_sums = (
+            [banks[r // 2][:, r % 2, :] for r in range(PACK)],
+            [banks[6][:, 0, :], banks[7][:, 0, :], banks[0][:, 0, :], banks[0][:, 1, :]],
+        )
+
+        nb_picked = sb.tile([P, N], F32, name="nb_picked")
+        nc.scalar.activation(nb_picked[:], nb_pool[:].indirect(offsets[:]), COPY)
+        nb_turned = banks[5][:].rearrange("p a (b c) -> p (a b) c", c=P)
         for r in range(PACK):
             nc.tensor.transpose(nb_turned[:, r, :], nb_picked[:, r:N:PACK], ident[:])
         bias = sb.tile([P, PACK], F32, name="bias")
         nc.scalar.copy(bias[:], nb_turned[:, :, BIAS_ROW])
 
-        q_bf = [sb.tile([P, cols.stop - cols.start, PACK], BF16, name="q_bf%d" % i, align_bytes=64) for i, (o, cols) in enumerate(pieces)]
-        q_codes = [sb.tile([P, NQ], U32, name="q_codes%d" % o, align_bytes=64) for o in range(PASSES)]
-        q_planes = [sb.tile([P, NQ], U8, name="q_plane%d" % o, align_bytes=64) for o in range(PASSES)]
+        q_bf = [[sb.tile([P, HALF, PACK], BF16, name="q_bf%d%d" % (h, o), tag=("last_queries" if (h, o) == (1, 1) else ""), align_bytes=64) for o in range(PASSES)] for h in range(2)]
+        q_codes = [[sb.tile([P, HALF], U32, name="q_codes%d%d" % (h, o), align_bytes=64) for o in range(PASSES)] for h in range(2)]
+        q_planes = [[sb.tile([P, HALF], U8, name="q_plane%d%d" % (h, o), align_bytes=64) for o in range(PASSES)] for h in range(2)]
 
-        def round_queries(engine_copy, i):
-            engine_copy(*interleave_views(q_bf[i][:], q_raw[i]))
+        def round_queries(engine_copy, h, o, cols):
+            engine_copy(*interleave_views(q_bf[h][o][:, cols, :], q_raw[h][o][:, :, cols]))
 
-        def quantise_queries(i):
-            o, cols = pieces[i]
-            nc.vector.quantize_mx(out=q_codes[o][:, cols].bitcast(FP8X4), scales=q_planes[o][:, cols], in_=q_bf[i][:].rearrange("p w j -> p (w j)"))
-
-        def gather_words(name, pool, tag):
-            picked = sb.tile([P, N], U32, name=name + "_picked", tag=tag)
-            nc.vector.tensor_copy(picked[:], pool[:].bitcast(U32).indirect(offsets[:]))
-            return picked[:].bitcast(U16).rearrange("p (s r o) -> p o s r", r=PACK, o=PASSES)
-
-        def deal_words(codes, halves, passes, tiles):
-            nc.vector.tensor_copy(codes[:].bitcast(U16).rearrange("p o r s -> p o s r")[:, passes, :, tiles], halves[:, passes, :, tiles])
+        def quantise_queries(h, o, cols):
+            nc.vector.quantize_mx(out=q_codes[h][o][:, cols].bitcast(FP8X4), scales=q_planes[h][o][:, cols], in_=q_bf[h][o][:, cols, :].rearrange("p w j -> p (w j)"))
 
         w_codes = [sb.tile([P, PASSES, PACK, 2 * P], U8, name="w_codes%d" % t, align_bytes=64) for t in range(2)]
-        round_queries(nc.scalar.copy, 0)
-        round_queries(nc.scalar.copy, 1)
-        quantise_queries(0)
-        k_halves = gather_words("k", k_pool, "")
-        quantise_queries(1)
-        deal_words(w_codes[GATE], k_halves, slice(0, 2), slice(0, 2))
-        deal_words(w_codes[GATE], k_halves, slice(0, 2), slice(2, PACK))
-        round_queries(nc.scalar.copy, 2)
-        quantise_queries(2)
 
-        def mx_pass(out, t, o, r, cols, start, stop):
+        def gather_words(t):
+            picked = sb.tile([P, N], U32, name="picked_words%d" % t)
+            nc.vector.tensor_copy(picked[:], word_pools[t][:].bitcast(U32).indirect(offsets[:]))
+            halves = picked[:].bitcast(U16).rearrange("p (s r o) -> p o s r", r=PACK, o=PASSES)
+            for tiles in (slice(0, 2), slice(2, PACK)):
+                nc.vector.tensor_copy(w_codes[t][:].bitcast(U16).rearrange("p o r s -> p o s r")[:, :, :, tiles], halves[:, :, :, tiles])
+
+        def mx_pass(out, t, o, r, h, cols, start, stop):
             nc.tensor.matmul_mx(
                 out=out,
                 lhsT=w_codes[t][:, o, r, :].bitcast(FP4X4),
                 lhsT_scale=planes[:, t, o, P * r : P * (r + 1)],
-                rhs=q_codes[o][:, cols].bitcast(FP8X4),
-                rhs_scale=q_planes[o][:, cols],
+                rhs=q_codes[h][o][:, cols].bitcast(FP8X4),
+                rhs_scale=q_planes[h][o][:, cols],
                 start=start,
                 stop=stop,
             )
 
-        gates = [[sb.tile([P, 2, HALF], F32, name="gates%d%d" % (h, pair), tag=("last_gates" if (h, pair) == (1, 1) else ""), align_bytes=64) for pair in range(2)] for h in range(2)]
+        whole, left, right = slice(0, HALF), slice(0, CHUNK), slice(CHUNK, HALF)
+        gates = [[sb.tile([P, 2, HALF], F32, name="gates%d%d" % (h, pair), tag={(0, 1): "q_raw11", (1, 1): "last_gates"}.get((h, pair), ""), align_bytes=64) for pair in range(2)] for h in range(2)]
 
-        def gate_passes(h, o):
-            for pair in range(2):
-                for i in range(4):
-                    r, c = 2 * pair + i // 2, 2 * h + i % 2
-                    mx_pass(gate_banks[2 * h + pair][:, i, :], GATE, o, r, slice(c * CHUNK, (c + 1) * CHUNK), o == 0 and i == 0, o == 1 and i == 3)
+        def activate(h, r, cols=whole):
+            nc.scalar.activation(gates[h][r // 2][:, r % 2, cols], gate_sums[h][r][:, cols], SILU, bias=bias[:, r : r + 1])
 
-        def activate(h):
+        def layer_sum(out, r, h, cols):
+            for o in (1, 0):
+                mx_pass(out, LIN, o, r, h, cols, o == 1, o == 0)
+
+        gather_words(GATE)
+        for cols in (left, right):
+            round_queries(nc.scalar.copy, 0, 0, cols)
+            quantise_queries(0, 0, cols)
             for r in range(PACK):
-                sums = gate_banks[2 * h + r // 2][:, 2 * (r % 2) : 2 * (r % 2) + 2, :].rearrange("p c q -> p (c q)")
-                nc.scalar.activation(gates[h][r // 2][:, r % 2, :], sums, SILU, bias=bias[:, r : r + 1])
+                mx_pass(gate_sums[0][r][:, cols], GATE, 0, r, 0, cols, cols == left and r % 2 == 0, False)
+        round_queries(nc.scalar.copy, 0, 1, left)
+        round_queries(nc.vector.tensor_copy, 0, 1, right)
+        quantise_queries(0, 1, whole)
+        for r in range(PACK):
+            mx_pass(gate_sums[0][r], GATE, 1, r, 0, whole, False, r % 2 == 1)
+        activate(0, 0)
+        activate(0, 1)
 
-        gate_passes(0, 0)
-        gate_passes(0, 1)
-        activate(0)
-        gate_passes(1, 0)
-
-        c_halves = gather_words("c", c_pool, "")
-        deal_words(w_codes[LIN], c_halves, slice(0, 2), slice(0, 2))
-        deal_words(w_codes[LIN], c_halves, slice(0, 2), slice(2, PACK))
-        round_queries(nc.vector.tensor_copy, 3)
-        quantise_queries(3)
+        gather_words(LIN)
+        for r in range(PACK):
+            layer_sum(banks[2 + r // 2][:, r % 2, :], r, 0, whole)
+        round_queries(nc.scalar.copy, 1, 0, whole)
+        round_queries(nc.scalar.copy, 1, 1, slice(0, 64))
+        round_queries(nc.vector.tensor_copy, 1, 1, slice(64, HALF))
+        quantise_queries(1, 0, whole)
+        quantise_queries(1, 1, whole)
+        activate(0, 2)
+        activate(0, 3)
+        for o in range(PASSES):
+            for r in range(2):
+                mx_pass(gate_sums[1][r], GATE, o, r, 1, whole, o == 0, o == 1)
+        for r in (2, 3):
+            for o in (1, 0):
+                mx_pass(gate_sums[1][r], GATE, o, r, 1, whole, o == 1, o == 0)
+        activate(1, 0)
+        activate(1, 1)
+        for cols in (left, right):
+            for r in (2, 3):
+                activate(1, r, cols)
 
         out_rows = out_0.rearrange("(p r) q -> p r q", r=PACK)
         words_out = out_1[0].rearrange("p q b -> p (q b)").bitcast(I32)
+        y = [sb.tile([P, PACK, HALF], F32, name="y%d" % h, tag=("" if h else "last_queries"), align_bytes=64) for h in range(2)]
+        y_bf = [sb.tile([P, HALF, PACK], BF16, name="y_bf%d" % h, align_bytes=64) for h in range(2)]
+        y_codes = [sb.tile([P, HALF], U32, name="y_codes%d" % h, tag=("" if h else "last_gates"), align_bytes=64) for h in range(2)]
         y_plane = sb.tile([P, NQ], U8, name="y_plane", align_bytes=64)
-        y = [sb.tile([P, PACK, HALF], F32, name="y%d" % h, tag=("" if h else "late")) for h in range(2)]
-        y_bf = sb.tile([P, NQ, PACK], BF16, name="y_bf", align_bytes=64)
-
-        def layer_sum(out, r, c):
-            for o in (1, 0):
-                mx_pass(out, LIN, o, r, slice(c * CHUNK, (c + 1) * CHUNK), o == 1, o == 0)
-
-        def gated_tile(bank, h, r):
-            for c in range(2):
-                layer_sum(bank[:, c, :], r, 2 * h + c)
-            nc.vector.tensor_tensor(y[h][:, r, :], bank[:, 0:2, :].rearrange("p c q -> p (c q)"), gates[h][r // 2][:, r % 2, :], MULT)
 
         def store_tiles(h, tiles):
             nc.sync.dma_start(out_rows[:, tiles, h * HALF : (h + 1) * HALF], y[h][:, tiles, :])
 
-        def gated_pair(bank, cols, c):
-            for r in (2, 3):
-                layer_sum(bank[:, r, :], r, c)
-            nc.vector.tensor_tensor(y[1][:, 2:PACK, cols], bank[:, 2:PACK, :], gates[1][1][:, :, cols], MULT)
-
         def round_result(engine_copy, h, cols, tiles):
-            engine_copy(*interleave_views(y_bf[:, h * HALF + cols.start : h * HALF + cols.stop, tiles], y[h][:, tiles, cols]))
+            engine_copy(*interleave_views(y_bf[h][:, cols, tiles], y[h][:, tiles, cols]))
 
-        def quantise_result(h):
-            cols = slice(h * HALF, (h + 1) * HALF)
-            nc.vector.quantize_mx(out=y_codes[h][:].bitcast(FP8X4), scales=y_plane[:, cols], in_=y_bf[:, cols, :].rearrange("p w j -> p (w j)"))
-            nc.sync.dma_start(words_out[:, cols], y_codes[h][:].bitcast(I32))
+        def quantise_result(h, cols):
+            plane = y_plane[:, h * HALF + cols.start : h * HALF + cols.stop]
+            nc.vector.quantize_mx(out=y_codes[h][:, cols].bitcast(FP8X4), scales=plane, in_=y_bf[h][:, cols, :].rearrange("p w j -> p (w j)"))
 
-        left, right = slice(0, CHUNK), slice(CHUNK, HALF)
-        for r in range(PACK):
-            gated_tile(lin_banks[r], 0, r)
-            if r % 2:
-                store_tiles(0, slice(r - 1, r + 1))
-        nc.gpsimd.tensor_scalar(y_bf[:, 0:192, :], y[0][:, :, 0:192].rearrange("p t c -> p c t"), 1.0, 0.0, MULT, ADD)
-        gate_passes(1, 1)
-        activate(1)
-        round_result(nc.scalar.copy, 0, slice(192, HALF), slice(0, PACK))
+        def store_codes(h):
+            nc.sync.dma_start(words_out[:, h * HALF : (h + 1) * HALF], y_codes[h][:].bitcast(I32))
+
+        for pair in range(2):
+            tiles = slice(2 * pair, 2 * pair + 2)
+            nc.vector.tensor_tensor(y[0][:, tiles, :], banks[2 + pair][:], gates[0][pair][:], MULT)
+            store_tiles(0, tiles)
+        nc.gpsimd.tensor_scalar(y_bf[0][:], y[0][:].rearrange("p t c -> p c t"), 1.0, 0.0, MULT, ADD)
+
         for r in range(2):
-            gated_tile(lin_banks[r], 1, r)
+            layer_sum(banks[4 + r][:, 0, :], r, 1, whole)
+            nc.vector.tensor_tensor(y[1][:, r, :], banks[4 + r][:, 0, :], gates[1][0][:, r, :], MULT)
         store_tiles(1, slice(0, 2))
-        round_result(nc.scalar.copy, 1, slice(0, HALF), slice(0, 2))
-        gated_pair(lin_banks[2], left, 2)
-        gated_pair(lin_banks[3], right, 3)
+        round_result(nc.scalar.copy, 1, left, slice(0, 2))
+        round_result(nc.scalar.copy, 1, right, slice(0, 2))
+        for bank, cols in ((banks[1], left), (banks[2], right)):
+            for r in (2, 3):
+                layer_sum(bank[:, r - 2, 0:CHUNK], r, 1, cols)
+            nc.vector.tensor_tensor(y[1][:, 2:PACK, cols], bank[:, :, 0:CHUNK], gates[1][1][:, :, cols], MULT)
         store_tiles(1, slice(2, PACK))
-        y_codes = [sb.tile([P, HALF], U32, name="y_codes%d" % h, tag=("" if h else "last_gates"), align_bytes=64) for h in range(2)]
         round_result(nc.vector.tensor_copy, 1, left, slice(2, PACK))
+        quantise_result(0, whole)
+        store_codes(0)
         round_result(nc.vector.tensor_copy, 1, right, slice(2, PACK))
-        quantise_result(0)
-        quantise_result(1)
+        quantise_result(1, left)
+        quantise_result(1, right)
+        store_codes(1)
         for quad in range(4):
             queue = nc.scalar if quad % 2 else nc.sync
             queue.dma_start(out_2[0, 4 * quad : 4 * quad + 4, :].bitcast(I32), y_plane[32 * quad : 32 * quad + 4, :].bitcast(I32))

@@ -74,9 +74,11 @@ def tile_attend_plh_bswiglu_topk_kernel(tc, qT, k_words, k_scales, c_words, c_sc
         load_queries(0, 0)
         load_queries(0, 1)
 
+        picked_scales = [sb.tile([P, N], U8, name="picked_scales%d" % t) for t in range(2)]
         dealt = [sb.tile([P, N], U8, name="dealt%d" % t) for t in range(2)]
         for t in range(2):
-            nc.vector.tensor_copy(dealt[t][:].rearrange("p (r s) -> p s r", r=PACK), scale_pools[t][:].indirect(offsets[:]))
+            nc.vector.tensor_copy(picked_scales[t][:], scale_pools[t][:].indirect(offsets[:]))
+            nc.vector.tensor_copy(dealt[t][:].rearrange("p (r s) -> p r s", r=PACK), picked_scales[t][:].rearrange("p (s r) -> p r s", r=PACK))
 
         def place_scales(t):
             for quad in (0, 2, 1, 3):
@@ -134,7 +136,9 @@ def tile_attend_plh_bswiglu_topk_kernel(tc, qT, k_words, k_scales, c_words, c_sc
             )
 
         whole, left, right = slice(0, HALF), slice(0, CHUNK), slice(CHUNK, HALF)
-        gates = [[sb.tile([P, 2, HALF], F32, name="gates%d%d" % (h, pair), tag={(0, 1): "q_raw11", (1, 1): "last_gates"}.get((h, pair), ""), align_bytes=64) for pair in range(2)] for h in range(2)]
+        first_gates = sb.tile([P, PACK, HALF], F32, name="first_gates", tag="q_raw11", align_bytes=64)
+        last_gates = [sb.tile([P, 2, HALF], F32, name="last_gates%d" % pair, tag=("last_gates" if pair else ""), align_bytes=64) for pair in range(2)]
+        gates = [[first_gates[:, 0:2, :], first_gates[:, 2:PACK, :]], last_gates]
 
         def activate(h, r, cols=whole):
             nc.scalar.activation(gates[h][r // 2][:, r % 2, cols], gate_sums[h][r][:, cols], SILU, bias=bias[:, r : r + 1])
@@ -144,18 +148,11 @@ def tile_attend_plh_bswiglu_topk_kernel(tc, qT, k_words, k_scales, c_words, c_sc
                 mx_pass(out, LIN, o, r, h, cols, o == 1, o == 0)
 
         gather_words(GATE)
-        for cols in (left, right):
-            round_queries(nc.scalar.copy, 0, 0, cols)
-            quantise_queries(0, 0, cols)
+        for o in range(PASSES):
+            round_queries(nc.scalar.copy, 0, o, whole)
+            quantise_queries(0, o, whole)
             for r in range(PACK):
-                mx_pass(gate_sums[0][r][:, cols], GATE, 0, r, 0, cols, cols == left and r % 2 == 0, False)
-        round_queries(nc.scalar.copy, 0, 1, left)
-        round_queries(nc.vector.tensor_copy, 0, 1, right)
-        quantise_queries(0, 1, whole)
-        for r in range(PACK):
-            mx_pass(gate_sums[0][r], GATE, 1, r, 0, whole, False, r % 2 == 1)
-        activate(0, 0)
-        activate(0, 1)
+                mx_pass(gate_sums[0][r], GATE, o, r, 0, whole, o == 0 and r % 2 == 0, o == 1 and r % 2 == 1)
 
         gather_words(LIN)
         for r in range(PACK):
@@ -165,8 +162,8 @@ def tile_attend_plh_bswiglu_topk_kernel(tc, qT, k_words, k_scales, c_words, c_sc
         round_queries(nc.vector.tensor_copy, 1, 1, slice(64, HALF))
         quantise_queries(1, 0, whole)
         quantise_queries(1, 1, whole)
-        activate(0, 2)
-        activate(0, 3)
+        for r in range(PACK):
+            activate(0, r)
         for o in range(PASSES):
             for r in range(2):
                 mx_pass(gate_sums[1][r], GATE, o, r, 1, whole, o == 0, o == 1)
@@ -201,7 +198,7 @@ def tile_attend_plh_bswiglu_topk_kernel(tc, qT, k_words, k_scales, c_words, c_sc
 
         for pair in range(2):
             tiles = slice(2 * pair, 2 * pair + 2)
-            nc.vector.tensor_tensor(y[0][:, tiles, :], banks[2 + pair][:], gates[0][pair][:], MULT)
+            nc.vector.tensor_tensor(y[0][:, tiles, :], banks[2 + pair][:], gates[0][pair], MULT)
             store_tiles(0, tiles)
         nc.gpsimd.tensor_scalar(y_bf[0][:], y[0][:].rearrange("p t c -> p c t"), 1.0, 0.0, MULT, ADD)
 

@@ -17,7 +17,6 @@ FP4X4 = mybir.dt.float4_e2m1fn_x4
 SILU = mybir.ActivationFunctionType.Silu
 COPY = mybir.ActivationFunctionType.Copy
 MULT = mybir.AluOpType.mult
-ADD = mybir.AluOpType.add
 
 P = 128
 PACK = 4
@@ -196,27 +195,29 @@ def tile_attend_plh_bswiglu_topk_kernel(tc, qT, k_words, k_scales, c_words, c_sc
         def store_codes(h):
             nc.sync.dma_start(words_out[:, h * HALF : (h + 1) * HALF], y_codes[h][:].bitcast(I32))
 
-        for pair in range(2):
-            tiles = slice(2 * pair, 2 * pair + 2)
-            nc.vector.tensor_tensor(y[0][:, tiles, :], banks[2 + pair][:], gates[0][pair], MULT)
-            store_tiles(0, tiles)
-        nc.gpsimd.tensor_scalar(y_bf[0][:], y[0][:].rearrange("p t c -> p c t"), 1.0, 0.0, MULT, ADD)
+        for cols in (left, right):
+            for pair in range(2):
+                tiles = slice(2 * pair, 2 * pair + 2)
+                nc.vector.tensor_tensor(y[0][:, tiles, cols], banks[2 + pair][:, :, cols], gates[0][pair][:, :, cols], MULT)
+                if cols == right:
+                    store_tiles(0, tiles)
+        round_result(nc.vector.tensor_copy, 0, left, slice(0, PACK))
 
         for r in range(2):
             layer_sum(banks[4 + r][:, 0, :], r, 1, whole)
             nc.vector.tensor_tensor(y[1][:, r, :], banks[4 + r][:, 0, :], gates[1][0][:, r, :], MULT)
         store_tiles(1, slice(0, 2))
-        round_result(nc.scalar.copy, 1, left, slice(0, 2))
-        round_result(nc.scalar.copy, 1, right, slice(0, 2))
         for bank, cols in ((banks[1], left), (banks[2], right)):
             for r in (2, 3):
                 layer_sum(bank[:, r - 2, 0:CHUNK], r, 1, cols)
             nc.vector.tensor_tensor(y[1][:, 2:PACK, cols], bank[:, :, 0:CHUNK], gates[1][1][:, :, cols], MULT)
         store_tiles(1, slice(2, PACK))
-        round_result(nc.vector.tensor_copy, 1, left, slice(2, PACK))
-        quantise_result(0, whole)
+        round_result(nc.scalar.copy, 0, right, slice(0, PACK))
+        round_result(nc.scalar.copy, 1, left, slice(0, PACK))
+        quantise_result(0, left)
+        round_result(nc.vector.tensor_copy, 1, right, slice(0, PACK))
+        quantise_result(0, right)
         store_codes(0)
-        round_result(nc.vector.tensor_copy, 1, right, slice(2, PACK))
         quantise_result(1, left)
         quantise_result(1, right)
         store_codes(1)

@@ -24,7 +24,7 @@ PASSES = 2
 HALF = NQ // 2
 CHUNK = 128
 BIAS_ROW = P - 1
-SCALE_ROWS = (96, 32)
+SCALE_ROW = 96
 GATE, LIN = 0, 1
 
 
@@ -43,15 +43,14 @@ def tile_attend_plh_bswiglu_topk_kernel(tc, qT, k_words, k_scales, c_words, c_sc
         word_pools = [sb.tile([P, T], I32, name="word_pool%d" % t, align_bytes=64) for t in range(2)]
         scale_pools = [sb.tile([P, T], U8, name="scale_pool%d" % t, align_bytes=64) for t in range(2)]
         q_raw = [[sb.tile([P, PACK, HALF], F32, name="q_raw%d%d" % (h, o), tag="q_raw%d%d" % (h, o), align_bytes=64) for o in range(PASSES)] for h in range(2)]
-        planes = sb.tile([P, 2, PASSES, N], U8, name="planes", align_bytes=64)
+        planes = sb.tile([P, PASSES, 2, N], U8, name="planes", align_bytes=64)
         ident = sb.tile([P, P], F32, name="ident")
 
         warm = sb.tile([P, 2], F32, name="warm")
         nc.gpsimd.memset(warm[:, 0:1], 0.0)
         nc.scalar.activation(warm[:, 1:2], warm[:, 0:1], SILU)
-        nc.gpsimd.memset(scale_pools[GATE][0:96, :].bitcast(I32), 0)
-        nc.gpsimd.memset(scale_pools[LIN][0:32, :].bitcast(I32), 0)
-        nc.gpsimd.memset(scale_pools[LIN][64:P, :].bitcast(I32), 0)
+        for pool in scale_pools:
+            nc.gpsimd.memset(pool[0:SCALE_ROW, :].bitcast(I32), 0)
         for cols in (slice(0, T - 1), slice(T - 1, T)):
             nc.vector.memset(nb_pool[0:BIAS_ROW, cols].bitcast(I32), 0)
         make_identity(nc, ident[:])
@@ -62,31 +61,29 @@ def tile_attend_plh_bswiglu_topk_kernel(tc, qT, k_words, k_scales, c_words, c_sc
         def load_queries(h, o):
             nc.sync.dma_start(q_raw[h][o][:], q_rows[o][:, :, h * HALF : (h + 1) * HALF])
 
-        def load_words(t, words):
-            nc.sync.dma_start(word_pools[t][:], words[0].rearrange("p t b -> p (t b)").bitcast(I32))
+        def load_words(t, words, cols):
+            nc.sync.dma_start(word_pools[t][:, cols], words[0].rearrange("p t b -> p (t b)").bitcast(I32)[:, cols])
 
-        nc.sync.dma_start(offsets[:], offs)
-        for queue, pool, scales, row in zip((nc.sync, nc.sync), scale_pools, (k_scales, c_scales), SCALE_ROWS):
-            queue.dma_start(pool[row : row + 32, :].bitcast(I32), scales.rearrange("o f t -> f o t").bitcast(I32))
+        for pool, scales in zip(scale_pools, (k_scales, c_scales)):
+            nc.sync.dma_start(pool[SCALE_ROW:P, :].bitcast(I32), scales.rearrange("o f t -> f o t").bitcast(I32))
         nc.sync.dma_start(nb_pool[BIAS_ROW:P, :], nb[0:1, :])
-        load_words(GATE, k_words)
+        nc.sync.dma_start(offsets[:], offs)
+        load_words(GATE, k_words, slice(0, T))
         load_queries(0, 0)
         load_queries(0, 1)
 
+        load_words(LIN, c_words, slice(0, T // 2))
+
         picked_scales = [sb.tile([P, N], U8, name="picked_scales%d" % t) for t in range(2)]
-        dealt = [sb.tile([P, N], U8, name="dealt%d" % t) for t in range(2)]
+        dealt = sb.tile([P, 2, N], U8, name="dealt")
         for t in range(2):
             nc.vector.tensor_copy(picked_scales[t][:], scale_pools[t][:].indirect(offsets[:]))
-            nc.vector.tensor_copy(dealt[t][:].rearrange("p (r s) -> p r s", r=PACK), picked_scales[t][:].rearrange("p (s r) -> p r s", r=PACK))
-
-        def place_scales(t):
-            for quad in (0, 2, 1, 3):
-                first = SCALE_ROWS[t] + 8 * quad
-                nc.sync.dma_start(planes[32 * quad : 32 * quad + 4, t].bitcast(I32), dealt[t][first : first + 8, :].bitcast(I32))
-
-        place_scales(GATE)
-        load_words(LIN, c_words)
-        place_scales(LIN)
+        for t in range(2):
+            nc.vector.tensor_copy(dealt[:, t, :].rearrange("p (r s) -> p r s", r=PACK), picked_scales[t][:].rearrange("p (s r) -> p r s", r=PACK))
+        for quad in (0, 2, 1, 3):
+            first = SCALE_ROW + 8 * quad
+            nc.sync.dma_start(planes[32 * quad : 32 * quad + 4].bitcast(I32), dealt[first : first + 8].bitcast(I32))
+        load_words(LIN, c_words, slice(T // 2, T))
         load_queries(1, 0)
         load_queries(1, 1)
 
@@ -127,7 +124,7 @@ def tile_attend_plh_bswiglu_topk_kernel(tc, qT, k_words, k_scales, c_words, c_sc
             nc.tensor.matmul_mx(
                 out=out,
                 lhsT=w_codes[t][:, o, r, :].bitcast(FP4X4),
-                lhsT_scale=planes[:, t, o, P * r : P * (r + 1)],
+                lhsT_scale=planes[:, o, t, P * r : P * (r + 1)],
                 rhs=q_codes[h][o][:, cols].bitcast(FP8X4),
                 rhs_scale=q_planes[h][o][:, cols],
                 start=start,

@@ -23,6 +23,7 @@ PACK = 4
 PASSES = 2
 HALF = NQ // 2
 CHUNK = 128
+SCALAR_QUERIES = 96
 BIAS_ROW = P - 1
 SCALE_ROW = 96
 GATE, LIN = 0, 1
@@ -36,13 +37,15 @@ def tile_attend_plh_bswiglu_topk_kernel(tc, qT, k_words, k_scales, c_words, c_sc
     nc = tc.nc
     with ExitStack() as ctx:
         sb = ctx.enter_context(tc.tile_pool(name="sb", bufs=1))
+        shared = ctx.enter_context(tc.tile_pool(name="shared", bufs=1))
         psum = ctx.enter_context(tc.psum_pool(name="psum", bufs=1))
 
         offsets = sb.tile([P, N // 16], U16, name="offsets")
         nb_pool = sb.tile([P, T], F32, name="nb_pool")
         word_pools = [sb.tile([P, T], I32, name="word_pool%d" % t, align_bytes=64) for t in range(2)]
         scale_pools = [sb.tile([P, T], U8, name="scale_pool%d" % t, align_bytes=64) for t in range(2)]
-        q_raw = [[sb.tile([P, PACK, HALF], F32, name="q_raw%d%d" % (h, o), tag="q_raw%d%d" % (h, o), align_bytes=64) for o in range(PASSES)] for h in range(2)]
+        q_raw = [[sb.tile([P, PACK, HALF], F32, name="q_raw0%d" % o) for o in range(PASSES)]]
+        q_raw.append([sb.tile([P, PACK, HALF], F32, name="q_raw10"), shared.tile([P, PACK, HALF], F32, name="q_raw11", offset=0)])
         planes = sb.tile([P, PASSES, 2, N], U8, name="planes", align_bytes=64)
         ident = sb.tile([P, P], F32, name="ident")
 
@@ -66,8 +69,8 @@ def tile_attend_plh_bswiglu_topk_kernel(tc, qT, k_words, k_scales, c_words, c_sc
 
         for pool, scales in zip(scale_pools, (k_scales, c_scales)):
             nc.sync.dma_start(pool[SCALE_ROW:P, :].bitcast(I32), scales.rearrange("o f t -> f o t").bitcast(I32))
-        nc.sync.dma_start(nb_pool[BIAS_ROW:P, :], nb[0:1, :])
         nc.sync.dma_start(offsets[:], offs)
+        nc.sync.dma_start(nb_pool[BIAS_ROW:P, :], nb[0:1, :])
         load_words(GATE, k_words, slice(0, T))
         load_queries(0, 0)
         load_queries(0, 1)
@@ -89,8 +92,8 @@ def tile_attend_plh_bswiglu_topk_kernel(tc, qT, k_words, k_scales, c_words, c_sc
 
         banks = [psum.tile([P, 2, HALF], F32, name="bank%d" % b) for b in range(8)]
         gate_sums = (
-            [banks[r // 2][:, r % 2, :] for r in range(PACK)],
-            [banks[6][:, 0, :], banks[7][:, 0, :], banks[0][:, 0, :], banks[0][:, 1, :]],
+            [banks[0][:, 0, :], banks[1][:, 0, :], banks[6][:, 0, :], banks[6][:, 1, :]],
+            [banks[7][:, 0, :], banks[0][:, 0, :], banks[1][:, 0, :], banks[1][:, 1, :]],
         )
 
         nb_picked = sb.tile([P, N], F32, name="nb_picked")
@@ -101,7 +104,7 @@ def tile_attend_plh_bswiglu_topk_kernel(tc, qT, k_words, k_scales, c_words, c_sc
         bias = sb.tile([P, PACK], F32, name="bias")
         nc.scalar.copy(bias[:], nb_turned[:, :, BIAS_ROW])
 
-        q_bf = [[sb.tile([P, HALF, PACK], BF16, name="q_bf%d%d" % (h, o), tag=("last_queries" if (h, o) == (1, 1) else ""), align_bytes=64) for o in range(PASSES)] for h in range(2)]
+        q_bf = [[sb.tile([P, HALF, PACK], BF16, name="q_bf%d%d" % (h, o), align_bytes=64) for o in range(PASSES)] for h in range(2)]
         q_codes = [[sb.tile([P, HALF], U32, name="q_codes%d%d" % (h, o), align_bytes=64) for o in range(PASSES)] for h in range(2)]
         q_planes = [[sb.tile([P, HALF], U8, name="q_plane%d%d" % (h, o), align_bytes=64) for o in range(PASSES)] for h in range(2)]
 
@@ -132,12 +135,16 @@ def tile_attend_plh_bswiglu_topk_kernel(tc, qT, k_words, k_scales, c_words, c_sc
             )
 
         whole, left, right = slice(0, HALF), slice(0, CHUNK), slice(CHUNK, HALF)
-        first_gates = sb.tile([P, PACK, HALF], F32, name="first_gates", tag="q_raw11", align_bytes=64)
+        early_gate = sb.tile([P, HALF], F32, name="early_gate")
+        first_gates = shared.tile([P, PACK - 1, HALF], F32, name="first_gates", offset=0)
         last_gates = [sb.tile([P, 2, HALF], F32, name="last_gates%d" % pair, tag=("last_gates" if pair else ""), align_bytes=64) for pair in range(2)]
-        gates = [[first_gates[:, 0:2, :], first_gates[:, 2:PACK, :]], last_gates]
+        gates = (
+            [early_gate[:]] + [first_gates[:, i, :] for i in range(PACK - 1)],
+            [last_gates[r // 2][:, r % 2, :] for r in range(PACK)],
+        )
 
         def activate(h, r, cols=whole):
-            nc.scalar.activation(gates[h][r // 2][:, r % 2, cols], gate_sums[h][r][:, cols], SILU, bias=bias[:, r : r + 1])
+            nc.scalar.activation(gates[h][r][:, cols], gate_sums[h][r][:, cols], SILU, bias=bias[:, r : r + 1])
 
         def layer_sum(out, r, h, cols):
             for o in (1, 0):
@@ -147,18 +154,20 @@ def tile_attend_plh_bswiglu_topk_kernel(tc, qT, k_words, k_scales, c_words, c_sc
         for o in range(PASSES):
             round_queries(nc.scalar.copy, 0, o, whole)
             quantise_queries(0, o, whole)
-            for r in range(PACK):
-                mx_pass(gate_sums[0][r], GATE, o, r, 0, whole, o == 0 and r % 2 == 0, o == 1 and r % 2 == 1)
+        for r in range(PACK):
+            for o in range(PASSES):
+                mx_pass(gate_sums[0][r], GATE, o, r, 0, whole, o == 0, o == 1)
+        activate(0, 0)
 
         gather_words(LIN)
         for r in range(PACK):
             layer_sum(banks[2 + r // 2][:, r % 2, :], r, 0, whole)
         round_queries(nc.scalar.copy, 1, 0, whole)
-        round_queries(nc.scalar.copy, 1, 1, slice(0, 64))
-        round_queries(nc.vector.tensor_copy, 1, 1, slice(64, HALF))
+        round_queries(nc.scalar.copy, 1, 1, slice(0, SCALAR_QUERIES))
+        round_queries(nc.vector.tensor_copy, 1, 1, slice(SCALAR_QUERIES, HALF))
         quantise_queries(1, 0, whole)
         quantise_queries(1, 1, whole)
-        for r in range(PACK):
+        for r in range(1, PACK):
             activate(0, r)
         for o in range(PASSES):
             for r in range(2):
@@ -174,9 +183,9 @@ def tile_attend_plh_bswiglu_topk_kernel(tc, qT, k_words, k_scales, c_words, c_sc
 
         out_rows = out_0.rearrange("(p r) q -> p r q", r=PACK)
         words_out = out_1[0].rearrange("p q b -> p (q b)").bitcast(I32)
-        y = [sb.tile([P, PACK, HALF], F32, name="y%d" % h, tag=("" if h else "last_queries"), align_bytes=64) for h in range(2)]
+        y = [shared.tile([P, PACK, HALF], F32, name="y0", offset=(PACK - 1) * HALF * 4), sb.tile([P, PACK, HALF], F32, name="y1")]
         y_bf = [sb.tile([P, HALF, PACK], BF16, name="y_bf%d" % h, align_bytes=64) for h in range(2)]
-        y_codes = [sb.tile([P, HALF], U32, name="y_codes%d" % h, tag=("" if h else "last_gates"), align_bytes=64) for h in range(2)]
+        y_codes = sb.tile([P, NQ], U32, name="y_codes", tag="last_gates", align_bytes=64)
         y_plane = sb.tile([P, NQ], U8, name="y_plane", align_bytes=64)
 
         def store_tiles(h, tiles):
@@ -186,38 +195,36 @@ def tile_attend_plh_bswiglu_topk_kernel(tc, qT, k_words, k_scales, c_words, c_sc
             engine_copy(*interleave_views(y_bf[h][:, cols, tiles], y[h][:, tiles, cols]))
 
         def quantise_result(h, cols):
-            plane = y_plane[:, h * HALF + cols.start : h * HALF + cols.stop]
-            nc.vector.quantize_mx(out=y_codes[h][:, cols].bitcast(FP8X4), scales=plane, in_=y_bf[h][:, cols, :].rearrange("p w j -> p (w j)"))
+            span = slice(h * HALF + cols.start, h * HALF + cols.stop)
+            nc.vector.quantize_mx(out=y_codes[:, span].bitcast(FP8X4), scales=y_plane[:, span], in_=y_bf[h][:, cols, :].rearrange("p w j -> p (w j)"))
 
-        def store_codes(h):
-            nc.sync.dma_start(words_out[:, h * HALF : (h + 1) * HALF], y_codes[h][:].bitcast(I32))
+        def store_codes(cols):
+            nc.sync.dma_start(words_out[:, cols], y_codes[:, cols].bitcast(I32))
 
-        for cols in (left, right):
-            for pair in range(2):
-                tiles = slice(2 * pair, 2 * pair + 2)
-                nc.vector.tensor_tensor(y[0][:, tiles, cols], banks[2 + pair][:, :, cols], gates[0][pair][:, :, cols], MULT)
-                if cols == right:
-                    store_tiles(0, tiles)
+        for r in range(PACK):
+            nc.vector.tensor_tensor(y[0][:, r, :], banks[2 + r // 2][:, r % 2, :], gates[0][r], MULT)
+            if r % 2:
+                store_tiles(0, slice(r - 1, r + 1))
         round_result(nc.vector.tensor_copy, 0, left, slice(0, PACK))
 
         for r in range(2):
             layer_sum(banks[4 + r][:, 0, :], r, 1, whole)
-            nc.vector.tensor_tensor(y[1][:, r, :], banks[4 + r][:, 0, :], gates[1][0][:, r, :], MULT)
+            nc.vector.tensor_tensor(y[1][:, r, :], banks[4 + r][:, 0, :], gates[1][r], MULT)
         store_tiles(1, slice(0, 2))
-        for bank, cols in ((banks[1], left), (banks[2], right)):
+        for bank, cols in ((banks[6], left), (banks[2], right)):
             for r in (2, 3):
                 layer_sum(bank[:, r - 2, 0:CHUNK], r, 1, cols)
-            nc.vector.tensor_tensor(y[1][:, 2:PACK, cols], bank[:, :, 0:CHUNK], gates[1][1][:, :, cols], MULT)
+            nc.vector.tensor_tensor(y[1][:, 2:PACK, cols], bank[:, :, 0:CHUNK], last_gates[1][:, :, cols], MULT)
         store_tiles(1, slice(2, PACK))
         round_result(nc.scalar.copy, 0, right, slice(0, PACK))
         round_result(nc.scalar.copy, 1, left, slice(0, PACK))
         quantise_result(0, left)
         round_result(nc.vector.tensor_copy, 1, right, slice(0, PACK))
         quantise_result(0, right)
-        store_codes(0)
         quantise_result(1, left)
+        store_codes(slice(0, NQ - CHUNK))
         quantise_result(1, right)
-        store_codes(1)
+        store_codes(slice(NQ - CHUNK, NQ))
         for quad in range(4):
             queue = nc.scalar if quad % 2 else nc.sync
             queue.dma_start(out_2[0, 4 * quad : 4 * quad + 4, :].bitcast(I32), y_plane[32 * quad : 32 * quad + 4, :].bitcast(I32))

from contextlib import ExitStack

import concourse.mybir as mybir
from concourse.masks import make_identity

N, T, D, NQ = 512, 2048, 1024, 512
FLOPS = 2 * 2 * N * NQ * D

F32 = mybir.dt.float32
BF16 = mybir.dt.bfloat16
I32 = mybir.dt.int32
U32 = mybir.dt.uint32
U16 = mybir.dt.uint16
U8 = mybir.dt.uint8
FP8X4 = mybir.dt.float8_e4m3fn_x4
FP4X4 = mybir.dt.float4_e2m1fn_x4
SILU = mybir.ActivationFunctionType.Silu
COPY = mybir.ActivationFunctionType.Copy
MULT = mybir.AluOpType.mult

P = 128
PACK = 4
PASSES = 2
HALF = NQ // 2
CHUNK = 128
SCALAR_QUERIES = 96
BIAS_ROW = P - 1
SCALE_ROW = 96
GATE, LIN = 0, 1


def interleave_views(dst, src):
    return (dst.rearrange("p (c i) t -> p c t i", i=4), src.rearrange("p t (c i) -> p c t i", i=4))


def tile_attend_plh_bswiglu_topk_kernel(tc, qT, k_words, k_scales, c_words, c_scales, nb, offs, out_0, out_1, out_2):
    nc = tc.nc
    with ExitStack() as ctx:
        sb = ctx.enter_context(tc.tile_pool(name="sb", bufs=1))
        shared = ctx.enter_context(tc.tile_pool(name="shared", bufs=1))
        psum = ctx.enter_context(tc.psum_pool(name="psum", bufs=1))

        offsets = sb.tile([P, N // 16], U16, name="offsets")
        nb_pool = sb.tile([P, T], F32, name="nb_pool")
        word_pools = [sb.tile([P, T], I32, name="word_pool%d" % t, align_bytes=64) for t in range(2)]
        scale_pools = [sb.tile([P, T], U8, name="scale_pool%d" % t, align_bytes=64) for t in range(2)]
        q_raw = [[sb.tile([P, PACK, HALF], F32, name="q_raw0%d" % o) for o in range(PASSES)]]
        q_raw.append([sb.tile([P, PACK, HALF], F32, name="q_raw10"), shared.tile([P, PACK, HALF], F32, name="q_raw11", offset=0)])
        planes = sb.tile([P, PASSES, 2, N], U8, name="planes", align_bytes=64)
        ident = sb.tile([P, P], F32, name="ident")

        warm = sb.tile([P, 2], F32, name="warm")
        nc.gpsimd.memset(warm[:, 0:1], 0.0)
        nc.scalar.activation(warm[:, 1:2], warm[:, 0:1], SILU)
        for pool in scale_pools:
            nc.gpsimd.memset(pool[0:SCALE_ROW, :].bitcast(I32), 0)
        for cols in (slice(0, T - 1), slice(T - 1, T)):
            nc.vector.memset(nb_pool[0:BIAS_ROW, cols].bitcast(I32), 0)
        make_identity(nc, ident[:])
        nc.gpsimd.memset(planes[:].bitcast(I32), 0)

        q_rows = qT[0].rearrange("(o p j) w -> o p j w", o=PASSES, j=PACK)

        def load_queries(h, o):
            nc.sync.dma_start(q_raw[h][o][:], q_rows[o][:, :, h * HALF : (h + 1) * HALF])

        def load_words(t, words, cols):
            nc.sync.dma_start(word_pools[t][:, cols], words[0].rearrange("p t b -> p (t b)").bitcast(I32)[:, cols])

        for pool, scales in zip(scale_pools, (k_scales, c_scales)):
            nc.sync.dma_start(pool[SCALE_ROW:P, :].bitcast(I32), scales.rearrange("o f t -> f o t").bitcast(I32))
        nc.sync.dma_start(offsets[:], offs)
        nc.sync.dma_start(nb_pool[BIAS_ROW:P, :], nb[0:1, :])
        load_words(GATE, k_words, slice(0, T))
        load_queries(0, 0)
        load_queries(0, 1)

        load_words(LIN, c_words, slice(0, T // 2))

        picked_scales = [sb.tile([P, N], U8, name="picked_scales%d" % t) for t in range(2)]
        dealt = sb.tile([P, 2, N], U8, name="dealt")
        for t in range(2):
            nc.vector.tensor_copy(picked_scales[t][:], scale_pools[t][:].indirect(offsets[:]))
        for t in range(2):
            nc.vector.tensor_copy(dealt[:, t, :].rearrange("p (r s) -> p r s", r=PACK), picked_scales[t][:].rearrange("p (s r) -> p r s", r=PACK))
        for quad in (0, 2, 1, 3):
            first = SCALE_ROW + 8 * quad
            nc.sync.dma_start(planes[32 * quad : 32 * quad + 4].bitcast(I32), dealt[first : first + 8].bitcast(I32))
        load_words(LIN, c_words, slice(T // 2, T))
        load_queries(1, 0)
        load_queries(1, 1)

        banks = [psum.tile([P, 2, HALF], F32, name="bank%d" % b) for b in range(8)]
        gate_sums = (
            [banks[0][:, 0, :], banks[1][:, 0, :], banks[6][:, 0, :], banks[6][:, 1, :]],
            [banks[7][:, 0, :], banks[0][:, 0, :], banks[1][:, 0, :], banks[1][:, 1, :]],
        )

        nb_picked = sb.tile([P, N], F32, name="nb_picked")
        nc.scalar.activation(nb_picked[:], nb_pool[:].indirect(offsets[:]), COPY)
        nb_turned = banks[5][:].rearrange("p a (b c) -> p (a b) c", c=P)
        for r in range(PACK):
            nc.tensor.transpose(nb_turned[:, r, :], nb_picked[:, r:N:PACK], ident[:])
        bias = sb.tile([P, PACK], F32, name="bias")
        nc.scalar.copy(bias[:], nb_turned[:, :, BIAS_ROW])

        q_bf = [[sb.tile([P, HALF, PACK], BF16, name="q_bf%d%d" % (h, o), align_bytes=64) for o in range(PASSES)] for h in range(2)]
        q_codes = [[sb.tile([P, HALF], U32, name="q_codes%d%d" % (h, o), align_bytes=64) for o in range(PASSES)] for h in range(2)]
        q_planes = [[sb.tile([P, HALF], U8, name="q_plane%d%d" % (h, o), align_bytes=64) for o in range(PASSES)] for h in range(2)]

        def round_queries(engine_copy, h, o, cols):
            engine_copy(*interleave_views(q_bf[h][o][:, cols, :], q_raw[h][o][:, :, cols]))

        def quantise_queries(h, o, cols):
            nc.vector.quantize_mx(out=q_codes[h][o][:, cols].bitcast(FP8X4), scales=q_planes[h][o][:, cols], in_=q_bf[h][o][:, cols, :].rearrange("p w j -> p (w j)"))

        w_codes = [sb.tile([P, PASSES, PACK, 2 * P], U8, name="w_codes%d" % t, align_bytes=64) for t in range(2)]

        def gather_words(t):
            picked = sb.tile([P, N], U32, name="picked_words%d" % t)
            nc.vector.tensor_copy(picked[:], word_pools[t][:].bitcast(U32).indirect(offsets[:]))
            halves = picked[:].bitcast(U16).rearrange("p (s r o) -> p o s r", r=PACK, o=PASSES)
            for tiles in (slice(0, 2), slice(2, PACK)):
                nc.vector.tensor_copy(w_codes[t][:].bitcast(U16).rearrange("p o r s -> p o s r")[:, :, :, tiles], halves[:, :, :, tiles])

        def mx_pass(out, t, o, r, h, cols, start, stop):
            nc.tensor.matmul_mx(
                out=out,
                lhsT=w_codes[t][:, o, r, :].bitcast(FP4X4),
                lhsT_scale=planes[:, o, t, P * r : P * (r + 1)],
                rhs=q_codes[h][o][:, cols].bitcast(FP8X4),
                rhs_scale=q_planes[h][o][:, cols],
                start=start,
                stop=stop,
            )

        whole, left, right = slice(0, HALF), slice(0, CHUNK), slice(CHUNK, HALF)
        early_gate = sb.tile([P, HALF], F32, name="early_gate")
        first_gates = shared.tile([P, PACK - 1, HALF], F32, name="first_gates", offset=0)
        last_gates = [sb.tile([P, 2, HALF], F32, name="last_gates%d" % pair, tag=("last_gates" if pair else ""), align_bytes=64) for pair in range(2)]
        gates = (
            [early_gate[:]] + [first_gates[:, i, :] for i in range(PACK - 1)],
            [last_gates[r // 2][:, r % 2, :] for r in range(PACK)],
        )

        def activate(h, r, cols=whole):
            nc.scalar.activation(gates[h][r][:, cols], gate_sums[h][r][:, cols], SILU, bias=bias[:, r : r + 1])

        def layer_sum(out, r, h, cols):
            for o in (1, 0):
                mx_pass(out, LIN, o, r, h, cols, o == 1, o == 0)

        gather_words(GATE)
        for o in range(PASSES):
            round_queries(nc.scalar.copy, 0, o, whole)
            quantise_queries(0, o, whole)
        for r in range(PACK):
            for o in range(PASSES):
                mx_pass(gate_sums[0][r], GATE, o, r, 0, whole, o == 0, o == 1)
        activate(0, 0)

        gather_words(LIN)
        for r in range(PACK):
            layer_sum(banks[2 + r // 2][:, r % 2, :], r, 0, whole)
        round_queries(nc.scalar.copy, 1, 0, whole)
        round_queries(nc.scalar.copy, 1, 1, slice(0, SCALAR_QUERIES))
        round_queries(nc.vector.tensor_copy, 1, 1, slice(SCALAR_QUERIES, HALF))
        quantise_queries(1, 0, whole)
        quantise_queries(1, 1, whole)
        for r in range(1, PACK):
            activate(0, r)
        for o in range(PASSES):
            for r in range(2):
                mx_pass(gate_sums[1][r], GATE, o, r, 1, whole, o == 0, o == 1)
        for r in (2, 3):
            for o in (1, 0):
                mx_pass(gate_sums[1][r], GATE, o, r, 1, whole, o == 1, o == 0)
        activate(1, 0)
        activate(1, 1)
        for cols in (left, right):
            for r in (2, 3):
                activate(1, r, cols)

        out_rows = out_0.rearrange("(p r) q -> p r q", r=PACK)
        words_out = out_1[0].rearrange("p q b -> p (q b)").bitcast(I32)
        y = [shared.tile([P, PACK, HALF], F32, name="y0", offset=(PACK - 1) * HALF * 4), sb.tile([P, PACK, HALF], F32, name="y1")]
        y_bf = [sb.tile([P, HALF, PACK], BF16, name="y_bf%d" % h, align_bytes=64) for h in range(2)]
        y_codes = sb.tile([P, NQ], U32, name="y_codes", tag="last_gates", align_bytes=64)
        y_plane = sb.tile([P, NQ], U8, name="y_plane", align_bytes=64)

        def store_tiles(h, tiles):
            nc.sync.dma_start(out_rows[:, tiles, h * HALF : (h + 1) * HALF], y[h][:, tiles, :])

        def round_result(engine_copy, h, cols, tiles):
            engine_copy(*interleave_views(y_bf[h][:, cols, tiles], y[h][:, tiles, cols]))

        def quantise_result(h, cols):
            span = slice(h * HALF + cols.start, h * HALF + cols.stop)
            nc.vector.quantize_mx(out=y_codes[:, span].bitcast(FP8X4), scales=y_plane[:, span], in_=y_bf[h][:, cols, :].rearrange("p w j -> p (w j)"))

        def store_codes(cols):
            nc.sync.dma_start(words_out[:, cols], y_codes[:, cols].bitcast(I32))

        for r in range(PACK):
            nc.vector.tensor_tensor(y[0][:, r, :], banks[2 + r // 2][:, r % 2, :], gates[0][r], MULT)
            if r % 2:
                store_tiles(0, slice(r - 1, r + 1))
        round_result(nc.vector.tensor_copy, 0, left, slice(0, PACK))

        for r in range(2):
            layer_sum(banks[4 + r][:, 0, :], r, 1, whole)
            nc.vector.tensor_tensor(y[1][:, r, :], banks[4 + r][:, 0, :], gates[1][r], MULT)
        store_tiles(1, slice(0, 2))
        for bank, cols in ((banks[6], left), (banks[2], right)):
            for r in (2, 3):
                layer_sum(bank[:, r - 2, 0:CHUNK], r, 1, cols)
            nc.vector.tensor_tensor(y[1][:, 2:PACK, cols], bank[:, :, 0:CHUNK], last_gates[1][:, :, cols], MULT)
        store_tiles(1, slice(2, PACK))
        round_result(nc.scalar.copy, 0, right, slice(0, PACK))
        round_result(nc.scalar.copy, 1, left, slice(0, PACK))
        quantise_result(0, left)
        round_result(nc.vector.tensor_copy, 1, right, slice(0, PACK))
        quantise_result(0, right)
        quantise_result(1, left)
        store_codes(slice(0, NQ - CHUNK))
        quantise_result(1, right)
        store_codes(slice(NQ - CHUNK, NQ))
        for quad in range(4):
            queue = nc.scalar if quad % 2 else nc.sync
            queue.dma_start(out_2[0, 4 * quad : 4 * quad + 4, :].bitcast(I32), y_plane[32 * quad : 32 * quad + 4, :].bitcast(I32))
